import numpy as np
import ml_dtypes


def mxq(x, axis, fmt="e4m3"):
    dtype, down = {"e4m3": (ml_dtypes.float8_e4m3fn, 7), "e5m2": (ml_dtypes.float8_e5m2, 14)}[fmt]
    v = np.moveaxis(np.asarray(x, np.float32).astype(ml_dtypes.bfloat16).astype(np.float64), axis, -1)
    blocks = v.reshape(v.shape[:-1] + (-1, 32))
    amax = np.abs(blocks).max(-1, keepdims=True)
    byte = np.maximum(np.where(amax > 0, np.frexp(amax)[1] - 1 + 127, 0) - down, 1)
    scale = np.exp2(byte - 127.0)
    codes = (blocks / scale).astype(np.float32).astype(dtype).astype(np.float64)
    return np.moveaxis((codes * scale).reshape(v.shape), -1, axis)


WIDE = False


def mx_kscale(k):
    if not WIDE:
        return np.ones(k)
    levels = np.array([10, -10, 5, -5, 0])
    if k % 512:
        return np.exp2(np.random.permutation(np.resize(levels, k // 32))).repeat(32)
    a = np.empty((k // 512, 16))
    for p in range(k // 512):
        a[p, :8] = np.random.permutation(np.resize(levels, 8))
        for g in range(8):
            far = levels[np.abs(levels - a[p, g]) >= 10]
            a[p, g + 8] = far[np.random.randint(len(far))]
    return np.exp2(a.ravel()).repeat(32)


def f64(x):
    return np.asarray(x).astype(np.float64)


def striped8(idx):
    return np.concatenate([v.reshape(-1, 16).T for v in idx]).astype(np.uint16)


def unstriped8(offs):
    return np.stack([offs[16 * g:16 * g + 16].T.reshape(-1) for g in range(8)]).astype(np.int64)


E2M1 = np.array([0.0, 0.5, 1.0, 1.5, 2.0, 3.0, 4.0, 6.0, -0.0, -0.5, -1.0, -1.5, -2.0, -3.0, -4.0, -6.0])


def pack_weight(w, fmt):
    k, n = w.shape
    w = f64(np.asarray(w, np.float32).astype(ml_dtypes.bfloat16)).reshape(k // 32, 32, n)
    amax = np.abs(w).max(1)
    if fmt == "e4m3":
        byte = np.frexp(amax)[1] - 1 + 127 - 7
    else:
        mant, ex = np.frexp(amax / 6.0)
        byte = np.where(mant > 0.5, ex, ex - 1) + 127
    byte = np.clip(np.where(amax > 0, byte, 1), 1, 254)
    scaled = (w * np.exp2(127.0 - byte)[:, None, :]).reshape(k, n).astype(np.float32)
    by_word = np.ascontiguousarray(scaled.reshape(k // 512, 128, 4, n).transpose(0, 1, 3, 2))
    if fmt == "e4m3":
        words = by_word.astype(ml_dtypes.float8_e4m3fn).view(np.uint8)
    else:
        c = by_word.astype(ml_dtypes.float4_e2m1fn).view(np.uint8) & 0xF
        words = (c[..., 0::2] | (c[..., 1::2] << 4)).reshape(k // 512, 128, 2 * n)
    return np.ascontiguousarray(words), np.ascontiguousarray(byte.astype(np.uint8).reshape(k // 512, 16, n))


def unpack_weight(words, scales, fmt):
    g, _, n = scales.shape
    words = np.ascontiguousarray(words).reshape(g, 128, n, -1)
    if fmt == "e4m3":
        vals = words.view(ml_dtypes.float8_e4m3fn).astype(np.float64)
    else:
        nib = np.empty((g, 128, n, 4), np.uint8)
        nib[..., 0::2] = words & 0xF
        nib[..., 1::2] = words >> 4
        vals = E2M1[nib]
    vals = vals * np.repeat(np.exp2(scales.astype(np.float64) - 127.0), 8, axis=1)[..., None]
    return vals.transpose(0, 1, 3, 2).reshape(g * 512, n)


K, R, M, T, S = 1024, 512, 1536, 1024, 512


def setup_inputs():
    n = np.random.standard_normal
    s = mx_kscale(K)[:, None]
    u = mx_kscale(R)[:, None]
    p_w4 = pack_weight(n((K, M)) / np.sqrt(K) / s, "e2m1")
    return {
        "xT": (n((K, T)) * s).astype(np.float32),
        "w4_words": p_w4[0],
        "w4_scales": p_w4[1],
        "down": (n((K, R)) / np.sqrt(K) / s * u.T).astype(np.float32),
        "up": (0.5 * n((R, M)) / np.sqrt(R) / u).astype(np.float32),
        "wgt": np.repeat(np.random.uniform(0.5, 2.0, (8, S)), 16, axis=0).astype(np.float32),
        "prev": (n((512, 1536))).astype(np.float32),
        "offs": striped8(np.stack([np.random.permutation(T)[:S] for _ in range(8)])),
    }


def reference(xT, w4_words, w4_scales, down, up, wgt, prev, offs):
    idx = unstriped8(offs)
    group = np.arange(K) % 512 // 64
    xg = f64(wgt)[np.arange(K) // 4 % 128] * f64(xT)[np.arange(K)[:, None], idx[group]]
    xT_ = mxq(xg, 0, "e4m3")
    w4_ = unpack_weight(w4_words, w4_scales, "e2m1")
    down_ = mxq(f64(down), 0, "e4m3")
    up_ = mxq(f64(up), 0, "e4m3")
    h_ = mxq(down_.T @ xT_, 0, "e4m3")
    y = xT_.T @ w4_ + h_.T @ up_
    return f64(prev) + y

@@ -1,0 +1,235 @@
+from contextlib import ExitStack
+
+import concourse.mybir as mybir
+
+K, R, M, T, S = 1024, 512, 1536, 1024, 512
+FLOPS = 2 * S * (K * R + K * M + R * M)
+
+F32 = mybir.dt.float32
+BF16 = mybir.dt.bfloat16
+I32 = mybir.dt.int32
+U32 = mybir.dt.uint32
+U16 = mybir.dt.uint16
+U8 = mybir.dt.uint8
+E4M3 = mybir.dt.float8_e4m3fn_x4
+E2M1 = mybir.dt.float4_e2m1fn_x4
+MULT = mybir.AluOpType.mult
+
+P = 128
+PASSES = K // 512
+HALF = S // 2
+NC = 512
+CHUNKS = M // NC
+JT = S // P
+
+
+def interleave(copy, out, in_):
+    copy(out=out.rearrange("p (c i) t -> p c t i", i=4), in_=in_.rearrange("p t (c i) -> p c t i", i=4))
+
+
+def tile_list_hlora_tm_res_kernel(tc, xT, w4_words, w4_scales, down, up, wgt, prev, offs, out):
+    nc = tc.nc
+    scopy = nc.scalar.copy
+    vcopy = nc.vector.tensor_copy
+    with ExitStack() as ctx:
+        sb = ctx.enter_context(tc.tile_pool(name="sb", bufs=1))
+        ps = ctx.enter_context(tc.psum_pool(name="ps", bufs=8))
+
+        lists = sb.tile([P, S // 16], U16, name="lists")
+        w4s = sb.tile([P, PASSES, M], U8, name="w4s", align_bytes=64)
+        nc.vector.memset(w4s[:].bitcast(I32), 0)
+        w4 = sb.tile([P, PASSES, 2 * M], U8, name="w4", align_bytes=64)
+        wg = sb.tile([P, S], F32, name="wg")
+        planes, draw, uraw, pv = {}, {}, {}, {}
+
+        def load_x(a, i):
+            planes[a, i] = sb.tile([P, T], F32, name=f"x{a}{i}")
+            rows = xT[512 * a : 512 * (a + 1), :].rearrange("(p i) t -> p i t", i=4)
+            nc.sync.dma_start(out=planes[a, i][:], in_=rows[:, i, :])
+
+        def load_down(a):
+            draw[a] = sb.tile([P, 4, R], F32, name=f"draw{a}")
+            nc.sync.dma_start(out=draw[a][:], in_=down[512 * a : 512 * (a + 1), :].rearrange("(p j) r -> p j r", j=4))
+
+        def load_up(c):
+            uraw[c] = sb.tile([P, 4, NC], F32, name=f"uraw{c}")
+            nc.sync.dma_start(out=uraw[c][:], in_=up[:, NC * c : NC * (c + 1)].rearrange("(p j) n -> p j n", j=4))
+
+        nc.sync.dma_start(lists[:], offs)
+        load_x(0, 0)
+        nc.sync.dma_start(out=wg[:], in_=wgt)
+        for i in range(1, 4):
+            load_x(0, i)
+        for i in range(4):
+            load_x(1, i)
+        for r in range(4):
+            nc.sync.dma_start(
+                out=w4s[r:P:32, :, :].bitcast(I32),
+                in_=w4_scales.bitcast(I32).rearrange("a (q r) n -> r q a n", r=4)[r],
+            )
+        nc.sync.dma_start(out=w4[:].bitcast(I32), in_=w4_words.bitcast(I32).rearrange("a p n -> p a n"))
+        load_down(0)
+        load_down(1)
+        for c in range(CHUNKS):
+            load_up(c)
+        for j in range(JT):
+            pv[j] = sb.tile([P, M], F32, name=f"prev{j}")
+            nc.sync.dma_start(out=pv[j][:], in_=prev[P * j : P * (j + 1), :])
+
+        xc, xs, gath, xb = {}, {}, {}, {}
+        for a in range(PASSES):
+            xc[a] = sb.tile([P, S], U32, name=f"xc{a}", align_bytes=64)
+            xs[a] = sb.tile([P, S], U8, name=f"xs{a}", align_bytes=64)
+            for h in range(2):
+                gath[a, h] = sb.tile([P, 4, HALF], F32, name=f"g{a}{h}")
+                xb[a, h] = sb.tile([P, HALF, 4], BF16, name=f"xb{a}{h}", align_bytes=64)
+
+        def gather(a, i, h):
+            nc.vector.tensor_tensor(
+                gath[a, h][:, i, :],
+                planes[a, i][:].indirect(lists[:, h * HALF // 16 : (h + 1) * HALF // 16]),
+                wg[:, h * HALF : (h + 1) * HALF],
+                MULT,
+            )
+
+        def quantize_x(a, h):
+            cols = slice(h * HALF, (h + 1) * HALF)
+            nc.vector.quantize_mx(
+                out=xc[a][:, cols].bitcast(E4M3), scales=xs[a][:, cols], in_=xb[a, h][:].rearrange("p j t -> p (j t)")
+            )
+
+        dc, ds, db = {}, {}, {}
+        for a in range(PASSES):
+            db[a] = sb.tile([P, R, 4], BF16, name=f"db{a}", align_bytes=64)
+            dc[a] = sb.tile([P, R], U32, name=f"dc{a}", align_bytes=64)
+            ds[a] = sb.tile([P, R], U8, name=f"ds{a}", align_bytes=64)
+
+        def cast_down(copy, a, lo, hi):
+            copy(
+                out=db[a][:].rearrange("p (t m) j -> p m t j", t=4)[:, lo:hi],
+                in_=draw[a][:].rearrange("p j (m t) -> p m t j", t=4)[:, lo:hi],
+            )
+
+        def quantize_down(a):
+            nc.vector.quantize_mx(
+                out=dc[a][:].bitcast(E4M3), scales=ds[a][:], in_=db[a][:].rearrange("p r j -> p (r j)")
+            )
+
+        ub, uc, us = [], [], []
+        for c in range(CHUNKS):
+            ub.append(sb.tile([P, NC, 4], BF16, name=f"ub{c}", align_bytes=64))
+            uc.append(sb.tile([P, NC], U32, name=f"uc{c}", align_bytes=64))
+            us.append(sb.tile([P, NC], U8, name=f"us{c}", align_bytes=64))
+
+        def cast_up(copy, c, lo, hi):
+            interleave(copy, ub[c][:, lo:hi, :], uraw[c][:, :, lo:hi])
+
+        def quantize_up(c):
+            nc.vector.quantize_mx(out=uc[c][:].bitcast(E4M3), scales=us[c][:], in_=ub[c][:].rearrange("p n j -> p (n j)"))
+
+        for i in range(4):
+            for h in range(2):
+                gather(0, i, h)
+        for h in range(2):
+            interleave(scopy, xb[0, h][:], gath[0, h][:])
+        for i in range(4):
+            for h in range(2):
+                gather(1, i, h)
+            if i in (1, 2):
+                quantize_x(0, i - 1)
+        interleave(scopy, xb[1, 0][:], gath[1, 0][:])
+        interleave(vcopy, xb[1, 1][:], gath[1, 1][:])
+        cast_down(scopy, 0, 0, P)
+        cast_down(vcopy, 1, 0, P)
+        quantize_x(1, 0)
+        quantize_x(1, 1)
+        quantize_down(0)
+        quantize_down(1)
+
+        acc = {}
+
+        def base(j, c):
+            acc[j, c] = ps.tile([P, NC], F32, name=f"acc{j}{c}", tag="bank")
+            for a in range(PASSES):
+                nc.tensor.matmul_mx(
+                    out=acc[j, c][:],
+                    lhsT=xc[a][:, P * j : P * (j + 1)].bitcast(E4M3),
+                    lhsT_scale=xs[a][:, P * j : P * (j + 1)],
+                    rhs=w4[:, a, 2 * NC * c : 2 * NC * (c + 1)].bitcast(E2M1),
+                    rhs_scale=w4s[:, a, NC * c : NC * (c + 1)],
+                    start=(a == 0),
+                    stop=False,
+                )
+
+        for j in range(2):
+            for c in range(CHUNKS):
+                base(j, c)
+
+        hc = sb.tile([P, S], U32, name="hc", align_bytes=64)
+        hs = sb.tile([P, S], U8, name="hs", align_bytes=64)
+        for j in range(JT):
+            cols = slice(P * j, P * (j + 1))
+            bank = ps.tile([P, 4, P], F32, name=f"h{j}", tag="bank")
+            for t in range(4):
+                for a in range(PASSES):
+                    nc.tensor.matmul_mx(
+                        out=bank[:, t, :],
+                        lhsT=dc[a][:, P * t : P * (t + 1)].bitcast(E4M3),
+                        lhsT_scale=ds[a][:, P * t : P * (t + 1)],
+                        rhs=xc[a][:, cols].bitcast(E4M3),
+                        rhs_scale=xs[a][:, cols],
+                        start=(a == 0),
+                        stop=(a == PASSES - 1),
+                    )
+            hb = sb.tile([P, P, 4], BF16, name=f"hb{j}", align_bytes=64)
+            scopy(out=hb[:], in_=bank[:].rearrange("p t j -> p j t"))
+            nc.vector.quantize_mx(
+                out=hc[:, cols].bitcast(E4M3), scales=hs[:, cols], in_=hb[:].rearrange("p j t -> p (j t)")
+            )
+
+        cast_up(scopy, 0, 0, NC)
+        cast_up(vcopy, 1, 0, NC)
+        quantize_up(0)
+        cast_up(scopy, 2, 0, NC // 2)
+        cast_up(vcopy, 2, NC // 2, NC)
+        quantize_up(1)
+        quantize_up(2)
+
+        base(2, 0)
+        base(2, 1)
+
+        def finish(j, c, res):
+            if (j, c) not in acc:
+                base(j, c)
+            nc.tensor.matmul_mx(
+                out=acc[j, c][:],
+                lhsT=hc[:, P * j : P * (j + 1)].bitcast(E4M3),
+                lhsT_scale=hs[:, P * j : P * (j + 1)],
+                rhs=uc[c][:].bitcast(E4M3),
+                rhs_scale=us[c][:],
+                start=False,
+                stop=True,
+            )
+            residual = pv[j][:, NC * c : NC * (c + 1)]
+            if (j, c) in ((1, 1), (2, 1), (3, 0)):
+                y = sb.tile([P, NC], F32, name=f"y{j}")
+                scopy(out=y[:], in_=acc[j, c][:])
+                nc.gpsimd.tensor_tensor(out=res, in0=y[:], in1=residual, op=mybir.AluOpType.add)
+            else:
+                nc.vector.tensor_add(out=res, in0=acc[j, c][:], in1=residual)
+
+        SPLIT = 2 * NC
+        for j in range(2):
+            left = sb.tile([P, SPLIT], F32, name=f"left{j}")
+            for c in range(2):
+                finish(j, c, left[:, NC * c : NC * (c + 1)])
+            nc.sync.dma_start(out=out[P * j : P * (j + 1), :SPLIT], in_=left[:])
+        right = sb.tile([P, 2, NC], F32, name="right")
+        for j in range(2):
+            finish(j, 2, right[:, j, :])
+        nc.sync.dma_start(out=out[: 2 * P, SPLIT:].rearrange("(j p) n -> p j n", p=P), in_=right[:])
+        for j in (2, 3):
+            res = sb.tile([P, M], F32, name=f"res{j}")
+            for c in range(CHUNKS):
+                finish(j, c, res[:, NC * c : NC * (c + 1)])
+            nc.sync.dma_start(out=out[P * j : P * (j + 1), :], in_=res[:])

@@ -33,14 +33,13 @@ def tile_list_hlora_tm_res_kernel(tc, xT, w4_words, w4_scales, down, up, wgt, pr
     vcopy = nc.vector.tensor_copy
     with ExitStack() as ctx:
         sb = ctx.enter_context(tc.tile_pool(name="sb", bufs=1))
-        ps = ctx.enter_context(tc.psum_pool(name="ps", bufs=8))
+        ps = ctx.enter_context(tc.psum_pool(name="ps", bufs=1))
 
         lists = sb.tile([P, S // 16], U16, name="lists")
         w4s = sb.tile([P, PASSES, M], U8, name="w4s", align_bytes=64)
         nc.vector.memset(w4s[:].bitcast(I32), 0)
-        w4 = sb.tile([P, PASSES, 2 * M], U8, name="w4", align_bytes=64)
         wg = sb.tile([P, S], F32, name="wg")
-        planes, draw, uraw, pv = {}, {}, {}, {}
+        planes, draw, w4, pv = {}, {}, {}, {}
 
         def load_x(a, i):
             planes[a, i] = sb.tile([P, T], F32, name=f"x{a}{i}")
@@ -51,9 +50,15 @@ def tile_list_hlora_tm_res_kernel(tc, xT, w4_words, w4_scales, down, up, wgt, pr
             draw[a] = sb.tile([P, 4, R], F32, name=f"draw{a}")
             nc.sync.dma_start(out=draw[a][:], in_=down[512 * a : 512 * (a + 1), :].rearrange("(p j) r -> p j r", j=4))
 
-        def load_up(c):
-            uraw[c] = sb.tile([P, 4, NC], F32, name=f"uraw{c}")
-            nc.sync.dma_start(out=uraw[c][:], in_=up[:, NC * c : NC * (c + 1)].rearrange("(p j) n -> p j n", j=4))
+        uraw = {}
+
+        def load_up(u):
+            uraw[u] = sb.tile([P, 2, M], F32, name=f"uraw{u}")
+            nc.sync.dma_start(out=uraw[u][:], in_=up.rearrange("(p j) n -> p j n", j=4)[:, 2 * u : 2 * u + 2, :])
+
+        def load_w4(a):
+            w4[a] = sb.tile([P, 2 * M], U8, name=f"w4{a}", align_bytes=64)
+            nc.sync.dma_start(out=w4[a][:].bitcast(I32), in_=w4_words.bitcast(I32)[a])
 
         nc.sync.dma_start(lists[:], offs)
         load_x(0, 0)
@@ -62,16 +67,18 @@ def tile_list_hlora_tm_res_kernel(tc, xT, w4_words, w4_scales, down, up, wgt, pr
             load_x(0, i)
         for i in range(4):
             load_x(1, i)
+            if i == 1:
+                load_down(0)
+        load_down(1)
+        load_up(0)
         for r in range(4):
             nc.sync.dma_start(
                 out=w4s[r:P:32, :, :].bitcast(I32),
                 in_=w4_scales.bitcast(I32).rearrange("a (q r) n -> r q a n", r=4)[r],
             )
-        nc.sync.dma_start(out=w4[:].bitcast(I32), in_=w4_words.bitcast(I32).rearrange("a p n -> p a n"))
-        load_down(0)
-        load_down(1)
-        for c in range(CHUNKS):
-            load_up(c)
+        load_w4(0)
+        load_up(1)
+        load_w4(1)
         for j in range(JT):
             pv[j] = sb.tile([P, M], F32, name=f"prev{j}")
             nc.sync.dma_start(out=pv[j][:], in_=prev[P * j : P * (j + 1), :])
@@ -80,17 +87,24 @@ def tile_list_hlora_tm_res_kernel(tc, xT, w4_words, w4_scales, down, up, wgt, pr
         for a in range(PASSES):
             xc[a] = sb.tile([P, S], U32, name=f"xc{a}", align_bytes=64)
             xs[a] = sb.tile([P, S], U8, name=f"xs{a}", align_bytes=64)
+            gath[a] = sb.tile([P, 4, S], F32, name=f"g{a}")
             for h in range(2):
-                gath[a, h] = sb.tile([P, 4, HALF], F32, name=f"g{a}{h}")
                 xb[a, h] = sb.tile([P, HALF, 4], BF16, name=f"xb{a}{h}", align_bytes=64)
 
-        def gather(a, i, h):
+        def gather(a, i, lo, hi):
             nc.vector.tensor_tensor(
-                gath[a, h][:, i, :],
-                planes[a, i][:].indirect(lists[:, h * HALF // 16 : (h + 1) * HALF // 16]),
-                wg[:, h * HALF : (h + 1) * HALF],
-                MULT,
+                gath[a][:, i, lo:hi], planes[a, i][:].indirect(lists[:, lo // 16 : hi // 16]), wg[:, lo:hi], MULT
             )
+
+        def gather_plane(a, i):
+            if i < 3:
+                gather(a, i, 0, S)
+            else:
+                gather(a, i, 0, HALF)
+                gather(a, i, HALF, S)
+
+        def cast_x(copy, a, h):
+            interleave(copy, xb[a, h][:], gath[a][:, :, h * HALF : (h + 1) * HALF])
 
         def quantize_x(a, h):
             cols = slice(h * HALF, (h + 1) * HALF)
@@ -121,55 +135,50 @@ def tile_list_hlora_tm_res_kernel(tc, xT, w4_words, w4_scales, down, up, wgt, pr
             uc.append(sb.tile([P, NC], U32, name=f"uc{c}", align_bytes=64))
             us.append(sb.tile([P, NC], U8, name=f"us{c}", align_bytes=64))
 
-        def cast_up(copy, c, lo, hi):
-            interleave(copy, ub[c][:, lo:hi, :], uraw[c][:, :, lo:hi])
+        def cast_up(copy, u, c, lo, hi):
+            interleave(copy, ub[c][:, lo:hi, 2 * u : 2 * u + 2], uraw[u][:, :, NC * c + lo : NC * c + hi])
 
         def quantize_up(c):
             nc.vector.quantize_mx(out=uc[c][:].bitcast(E4M3), scales=us[c][:], in_=ub[c][:].rearrange("p n j -> p (n j)"))
 
         for i in range(4):
-            for h in range(2):
-                gather(0, i, h)
+            gather_plane(0, i)
         for h in range(2):
-            interleave(scopy, xb[0, h][:], gath[0, h][:])
+            cast_x(scopy, 0, h)
+        cast_down(scopy, 0, 0, P)
         for i in range(4):
-            for h in range(2):
-                gather(1, i, h)
+            gather_plane(1, i)
             if i in (1, 2):
                 quantize_x(0, i - 1)
-        interleave(scopy, xb[1, 0][:], gath[1, 0][:])
-        interleave(vcopy, xb[1, 1][:], gath[1, 1][:])
-        cast_down(scopy, 0, 0, P)
-        cast_down(vcopy, 1, 0, P)
+        cast_x(scopy, 1, 0)
+        cast_x(vcopy, 1, 1)
+        quantize_down(0)
         quantize_x(1, 0)
         quantize_x(1, 1)
-        quantize_down(0)
+        cast_down(scopy, 1, 0, 96)
+        cast_down(vcopy, 1, 96, P)
         quantize_down(1)
 
         acc = {}
 
-        def base(j, c):
-            acc[j, c] = ps.tile([P, NC], F32, name=f"acc{j}{c}", tag="bank")
-            for a in range(PASSES):
-                nc.tensor.matmul_mx(
-                    out=acc[j, c][:],
-                    lhsT=xc[a][:, P * j : P * (j + 1)].bitcast(E4M3),
-                    lhsT_scale=xs[a][:, P * j : P * (j + 1)],
-                    rhs=w4[:, a, 2 * NC * c : 2 * NC * (c + 1)].bitcast(E2M1),
-                    rhs_scale=w4s[:, a, NC * c : NC * (c + 1)],
-                    start=(a == 0),
-                    stop=False,
-                )
-
-        for j in range(2):
-            for c in range(CHUNKS):
-                base(j, c)
+        def base(j, c, a):
+            if a == 0:
+                acc[j, c] = ps.tile([P, NC], F32, name=f"acc{j}{c}", tag=f"bank{(CHUNKS * j + c) % 8}")
+            nc.tensor.matmul_mx(
+                out=acc[j, c][:],
+                lhsT=xc[a][:, P * j : P * (j + 1)].bitcast(E4M3),
+                lhsT_scale=xs[a][:, P * j : P * (j + 1)],
+                rhs=w4[a][:, 2 * NC * c : 2 * NC * (c + 1)].bitcast(E2M1),
+                rhs_scale=w4s[:, a, NC * c : NC * (c + 1)],
+                start=(a == 0),
+                stop=False,
+            )
 
         hc = sb.tile([P, S], U32, name="hc", align_bytes=64)
         hs = sb.tile([P, S], U8, name="hs", align_bytes=64)
         for j in range(JT):
             cols = slice(P * j, P * (j + 1))
-            bank = ps.tile([P, 4, P], F32, name=f"h{j}", tag="bank")
+            bank = ps.tile([P, 4, P], F32, name=f"h{j}", tag=f"bank{4 + j}")
             for t in range(4):
                 for a in range(PASSES):
                     nc.tensor.matmul_mx(
@@ -187,20 +196,26 @@ def tile_list_hlora_tm_res_kernel(tc, xT, w4_words, w4_scales, down, up, wgt, pr
                 out=hc[:, cols].bitcast(E4M3), scales=hs[:, cols], in_=hb[:].rearrange("p j t -> p (j t)")
             )
 
-        cast_up(scopy, 0, 0, NC)
-        cast_up(vcopy, 1, 0, NC)
+        early = [(j, c) for j in range(JT) for c in range(CHUNKS)][:8]
+        for j, c in early:
+            base(j, c, 0)
+
+        for c in range(CHUNKS):
+            cast_up(vcopy, 0, c, 0, NC)
+        cast_up(scopy, 1, 0, 0, 128)
+        cast_up(vcopy, 1, 0, 128, NC)
+        cast_up(scopy, 1, 1, 0, 320)
+        cast_up(vcopy, 1, 1, 320, NC)
         quantize_up(0)
-        cast_up(scopy, 2, 0, NC // 2)
-        cast_up(vcopy, 2, NC // 2, NC)
+        cast_up(scopy, 1, 2, 0, 320)
+        cast_up(vcopy, 1, 2, 320, NC)
         quantize_up(1)
         quantize_up(2)
 
-        base(2, 0)
-        base(2, 1)
-
         def finish(j, c, res):
-            if (j, c) not in acc:
-                base(j, c)
+            if (j, c) not in early:
+                base(j, c, 0)
+                base(j, c, 1)
             nc.tensor.matmul_mx(
                 out=acc[j, c][:],
                 lhsT=hc[:, P * j : P * (j + 1)].bitcast(E4M3),
@@ -211,25 +226,19 @@ def tile_list_hlora_tm_res_kernel(tc, xT, w4_words, w4_scales, down, up, wgt, pr
                 stop=True,
             )
             residual = pv[j][:, NC * c : NC * (c + 1)]
-            if (j, c) in ((1, 1), (2, 1), (3, 0)):
+            if c == 0:
                 y = sb.tile([P, NC], F32, name=f"y{j}")
                 scopy(out=y[:], in_=acc[j, c][:])
                 nc.gpsimd.tensor_tensor(out=res, in0=y[:], in1=residual, op=mybir.AluOpType.add)
             else:
                 nc.vector.tensor_add(out=res, in0=acc[j, c][:], in1=residual)
 
-        SPLIT = 2 * NC
-        for j in range(2):
-            left = sb.tile([P, SPLIT], F32, name=f"left{j}")
-            for c in range(2):
-                finish(j, c, left[:, NC * c : NC * (c + 1)])
-            nc.sync.dma_start(out=out[P * j : P * (j + 1), :SPLIT], in_=left[:])
-        right = sb.tile([P, 2, NC], F32, name="right")
-        for j in range(2):
-            finish(j, 2, right[:, j, :])
-        nc.sync.dma_start(out=out[: 2 * P, SPLIT:].rearrange("(j p) n -> p j n", p=P), in_=right[:])
-        for j in (2, 3):
+        waiting = list(early)
+        for j in range(JT):
             res = sb.tile([P, M], F32, name=f"res{j}")
             for c in range(CHUNKS):
+                for ahead in waiting[: 4 if c == 0 else 2]:
+                    base(*ahead, 1)
+                    waiting.remove(ahead)
                 finish(j, c, res[:, NC * c : NC * (c + 1)])
             nc.sync.dma_start(out=out[P * j : P * (j + 1), :], in_=res[:])

@@ -37,8 +37,11 @@ def tile_list_hlora_tm_res_kernel(tc, xT, w4_words, w4_scales, down, up, wgt, pr
 
         lists = sb.tile([P, S // 16], U16, name="lists")
         w4s = sb.tile([P, PASSES, M], U8, name="w4s", align_bytes=64)
+        rows8 = sb.tile([P, S], F32, name="rows8", align_bytes=64)
+        for quad in range(4):
+            (nc.vector if quad < 2 else nc.gpsimd).memset(rows8[32 * quad : 32 * quad + 30, :], 0.0)
         nc.vector.memset(w4s[:].bitcast(I32), 0)
-        wg = sb.tile([P, S], F32, name="wg")
+        wg = sb.tile([P, S], F32, name="wg", align_bytes=64)
         planes, draw, w4, pv = {}, {}, {}, {}
 
         def load_x(a, i):
@@ -50,38 +53,51 @@ def tile_list_hlora_tm_res_kernel(tc, xT, w4_words, w4_scales, down, up, wgt, pr
             draw[a] = sb.tile([P, 4, R], F32, name=f"draw{a}")
             nc.sync.dma_start(out=draw[a][:], in_=down[512 * a : 512 * (a + 1), :].rearrange("(p j) r -> p j r", j=4))
 
-        uraw = {}
-
-        def load_up(u):
-            uraw[u] = sb.tile([P, 2, M], F32, name=f"uraw{u}")
-            nc.sync.dma_start(out=uraw[u][:], in_=up.rearrange("(p j) n -> p j n", j=4)[:, 2 * u : 2 * u + 2, :])
-
         def load_w4(a):
             w4[a] = sb.tile([P, 2 * M], U8, name=f"w4{a}", align_bytes=64)
             nc.sync.dma_start(out=w4[a][:].bitcast(I32), in_=w4_words.bitcast(I32)[a])
 
-        nc.sync.dma_start(lists[:], offs)
         load_x(0, 0)
-        nc.sync.dma_start(out=wg[:], in_=wgt)
+        for e in range(2):
+            nc.sync.dma_start(out=rows8[30 + e : P : 32, :], in_=wgt[16 * e : P : 32, :])
+        nc.sync.dma_start(lists[:], offs)
         for i in range(1, 4):
             load_x(0, i)
         for i in range(4):
             load_x(1, i)
             if i == 1:
                 load_down(0)
-        load_down(1)
-        load_up(0)
         for r in range(4):
             nc.sync.dma_start(
                 out=w4s[r:P:32, :, :].bitcast(I32),
                 in_=w4_scales.bitcast(I32).rearrange("a (q r) n -> r q a n", r=4)[r],
             )
         load_w4(0)
-        load_up(1)
         load_w4(1)
+        load_down(1)
+        uraw = {}
+        cuts = (0, 512, 1024, 1536)
+        for lo, hi in zip(cuts, cuts[1:]):
+            part = sb.tile([P, 4, hi - lo], F32, name=f"uraw{lo}")
+            nc.sync.dma_start(out=part[:], in_=up[:, lo:hi].rearrange("(p j) n -> p j n", j=4))
+            for c in range(lo // NC, hi // NC):
+                uraw[c] = part[:, :, NC * c - lo : NC * (c + 1) - lo]
         for j in range(JT):
             pv[j] = sb.tile([P, M], F32, name=f"prev{j}")
             nc.sync.dma_start(out=pv[j][:], in_=prev[P * j : P * (j + 1), :])
+
+        turned = sb.tile([P, S], F32, name="turned", align_bytes=64)
+        spread = sb.tile([P, S], F32, name="spread", align_bytes=64)
+        halves = [slice(h * HALF, (h + 1) * HALF) for h in range(2)]
+        for cols in halves:
+            nc.vector.transpose(turned[:, cols], rows8[:, cols])
+        for cols in halves:
+            vcopy(
+                out=spread[:, cols].rearrange("p (b e s) -> p b e s", e=2, s=16),
+                in_=turned[:, cols].rearrange("p (b e s) -> p b e s", e=32, s=1)[:, :, 30:32, :].to_broadcast([P, HALF // 32, 2, 16]),
+            )
+        for cols in halves:
+            nc.vector.transpose(wg[:, cols], spread[:, cols])
 
         xc, xs, gath, xb = {}, {}, {}, {}
         for a in range(PASSES):
@@ -135,8 +151,8 @@ def tile_list_hlora_tm_res_kernel(tc, xT, w4_words, w4_scales, down, up, wgt, pr
             uc.append(sb.tile([P, NC], U32, name=f"uc{c}", align_bytes=64))
             us.append(sb.tile([P, NC], U8, name=f"us{c}", align_bytes=64))
 
-        def cast_up(copy, u, c, lo, hi):
-            interleave(copy, ub[c][:, lo:hi, 2 * u : 2 * u + 2], uraw[u][:, :, NC * c + lo : NC * c + hi])
+        def cast_up(copy, c, lo, hi):
+            interleave(copy, ub[c][:, lo:hi, :], uraw[c][:, :, lo:hi])
 
         def quantize_up(c):
             nc.vector.quantize_mx(out=uc[c][:].bitcast(E4M3), scales=us[c][:], in_=ub[c][:].rearrange("p n j -> p (n j)"))
@@ -174,11 +190,16 @@ def tile_list_hlora_tm_res_kernel(tc, xT, w4_words, w4_scales, down, up, wgt, pr
                 stop=False,
             )
 
+        early = [(j, c) for j in range(JT) for c in range(CHUNKS)][:8]
+        for a in range(PASSES):
+            for j, c in early[:4]:
+                base(j, c, a)
+
         hc = sb.tile([P, S], U32, name="hc", align_bytes=64)
         hs = sb.tile([P, S], U8, name="hs", align_bytes=64)
         for j in range(JT):
             cols = slice(P * j, P * (j + 1))
-            bank = ps.tile([P, 4, P], F32, name=f"h{j}", tag=f"bank{4 + j}")
+            bank = ps.tile([P, 4, P], F32, name=f"h{j}", tag=f"bank{4 + j % 4}")
             for t in range(4):
                 for a in range(PASSES):
                     nc.tensor.matmul_mx(
@@ -196,21 +217,14 @@ def tile_list_hlora_tm_res_kernel(tc, xT, w4_words, w4_scales, down, up, wgt, pr
                 out=hc[:, cols].bitcast(E4M3), scales=hs[:, cols], in_=hb[:].rearrange("p j t -> p (j t)")
             )
 
-        early = [(j, c) for j in range(JT) for c in range(CHUNKS)][:8]
-        for j, c in early:
+        for j, c in early[4:]:
             base(j, c, 0)
+            base(j, c, 1)
 
-        for c in range(CHUNKS):
-            cast_up(vcopy, 0, c, 0, NC)
-        cast_up(scopy, 1, 0, 0, 128)
-        cast_up(vcopy, 1, 0, 128, NC)
-        cast_up(scopy, 1, 1, 0, 320)
-        cast_up(vcopy, 1, 1, 320, NC)
-        quantize_up(0)
-        cast_up(scopy, 1, 2, 0, 320)
-        cast_up(vcopy, 1, 2, 320, NC)
-        quantize_up(1)
-        quantize_up(2)
+        for c, share in enumerate((256, 192, 256)):
+            cast_up(scopy, c, 0, share)
+            cast_up(vcopy, c, share, NC)
+            quantize_up(c)
 
         def finish(j, c, res):
             if (j, c) not in early:
@@ -226,19 +240,25 @@ def tile_list_hlora_tm_res_kernel(tc, xT, w4_words, w4_scales, down, up, wgt, pr
                 stop=True,
             )
             residual = pv[j][:, NC * c : NC * (c + 1)]
-            if c == 0:
-                y = sb.tile([P, NC], F32, name=f"y{j}")
+            if (j, c) in ((1, 0), (2, 0), (3, 0)):
+                y = sb.tile([P, NC], F32, name=f"y{j}{c}")
                 scopy(out=y[:], in_=acc[j, c][:])
                 nc.gpsimd.tensor_tensor(out=res, in0=y[:], in1=residual, op=mybir.AluOpType.add)
             else:
                 nc.vector.tensor_add(out=res, in0=acc[j, c][:], in1=residual)
 
-        waiting = list(early)
-        for j in range(JT):
+        SPLIT = 2 * NC
+        for j in range(2):
+            left = sb.tile([P, SPLIT], F32, name=f"left{j}")
+            for c in range(2):
+                finish(j, c, left[:, NC * c : NC * (c + 1)])
+            nc.sync.dma_start(out=out[P * j : P * (j + 1), :SPLIT], in_=left[:])
+        right = sb.tile([P, 2, NC], F32, name="right")
+        for j in range(2):
+            finish(j, 2, right[:, j, :])
+        nc.sync.dma_start(out=out[: 2 * P, SPLIT:].rearrange("(j p) n -> p j n", p=P), in_=right[:])
+        for j in (2, 3):
             res = sb.tile([P, M], F32, name=f"res{j}")
             for c in range(CHUNKS):
-                for ahead in waiting[: 4 if c == 0 else 2]:
-                    base(*ahead, 1)
-                    waiting.remove(ahead)
                 finish(j, c, res[:, NC * c : NC * (c + 1)])
             nc.sync.dma_start(out=out[P * j : P * (j + 1), :], in_=res[:])

@@ -37,11 +37,8 @@ def tile_list_hlora_tm_res_kernel(tc, xT, w4_words, w4_scales, down, up, wgt, pr
 
         lists = sb.tile([P, S // 16], U16, name="lists")
         w4s = sb.tile([P, PASSES, M], U8, name="w4s", align_bytes=64)
-        rows8 = sb.tile([P, S], F32, name="rows8", align_bytes=64)
-        for quad in range(4):
-            (nc.vector if quad < 2 else nc.gpsimd).memset(rows8[32 * quad : 32 * quad + 30, :], 0.0)
         nc.vector.memset(w4s[:].bitcast(I32), 0)
-        wg = sb.tile([P, S], F32, name="wg", align_bytes=64)
+        wg = sb.tile([P, S], F32, name="wg")
         planes, draw, w4, pv = {}, {}, {}, {}
 
         def load_x(a, i):
@@ -57,10 +54,9 @@ def tile_list_hlora_tm_res_kernel(tc, xT, w4_words, w4_scales, down, up, wgt, pr
             w4[a] = sb.tile([P, 2 * M], U8, name=f"w4{a}", align_bytes=64)
             nc.sync.dma_start(out=w4[a][:].bitcast(I32), in_=w4_words.bitcast(I32)[a])
 
-        load_x(0, 0)
-        for e in range(2):
-            nc.sync.dma_start(out=rows8[30 + e : P : 32, :], in_=wgt[16 * e : P : 32, :])
         nc.sync.dma_start(lists[:], offs)
+        load_x(0, 0)
+        nc.sync.dma_start(out=wg[:], in_=wgt)
         for i in range(1, 4):
             load_x(0, i)
         for i in range(4):
@@ -85,19 +81,6 @@ def tile_list_hlora_tm_res_kernel(tc, xT, w4_words, w4_scales, down, up, wgt, pr
         for j in range(JT):
             pv[j] = sb.tile([P, M], F32, name=f"prev{j}")
             nc.sync.dma_start(out=pv[j][:], in_=prev[P * j : P * (j + 1), :])
-
-        turned = sb.tile([P, S], F32, name="turned", align_bytes=64)
-        spread = sb.tile([P, S], F32, name="spread", align_bytes=64)
-        halves = [slice(h * HALF, (h + 1) * HALF) for h in range(2)]
-        for cols in halves:
-            nc.vector.transpose(turned[:, cols], rows8[:, cols])
-        for cols in halves:
-            vcopy(
-                out=spread[:, cols].rearrange("p (b e s) -> p b e s", e=2, s=16),
-                in_=turned[:, cols].rearrange("p (b e s) -> p b e s", e=32, s=1)[:, :, 30:32, :].to_broadcast([P, HALF // 32, 2, 16]),
-            )
-        for cols in halves:
-            nc.vector.transpose(wg[:, cols], spread[:, cols])
 
         xc, xs, gath, xb = {}, {}, {}, {}
         for a in range(PASSES):

@@ -57,18 +57,20 @@ def tile_list_hlora_tm_res_kernel(tc, xT, w4_words, w4_scales, down, up, wgt, pr
         nc.sync.dma_start(lists[:], offs)
         load_x(0, 0)
         nc.sync.dma_start(out=wg[:], in_=wgt)
-        for i in range(1, 4):
-            load_x(0, i)
-        for i in range(4):
-            load_x(1, i)
-            if i == 1:
-                load_down(0)
+        load_x(0, 1)
+        load_x(0, 2)
+        load_x(0, 3)
+        load_x(1, 0)
+        load_x(1, 1)
         for r in range(4):
             nc.sync.dma_start(
                 out=w4s[r:P:32, :, :].bitcast(I32),
                 in_=w4_scales.bitcast(I32).rearrange("a (q r) n -> r q a n", r=4)[r],
             )
         load_w4(0)
+        load_x(1, 2)
+        load_x(1, 3)
+        load_down(0)
         load_w4(1)
         load_down(1)
         uraw = {}
@@ -144,18 +146,17 @@ def tile_list_hlora_tm_res_kernel(tc, xT, w4_words, w4_scales, down, up, wgt, pr
             gather_plane(0, i)
         for h in range(2):
             cast_x(scopy, 0, h)
-        cast_down(scopy, 0, 0, P)
         for i in range(4):
             gather_plane(1, i)
             if i in (1, 2):
                 quantize_x(0, i - 1)
         cast_x(scopy, 1, 0)
         cast_x(vcopy, 1, 1)
-        quantize_down(0)
         quantize_x(1, 0)
+        cast_down(vcopy, 0, 0, P)
         quantize_x(1, 1)
-        cast_down(scopy, 1, 0, 96)
-        cast_down(vcopy, 1, 96, P)
+        cast_down(vcopy, 1, 0, P)
+        quantize_down(0)
         quantize_down(1)
 
         acc = {}
@@ -175,14 +176,14 @@ def tile_list_hlora_tm_res_kernel(tc, xT, w4_words, w4_scales, down, up, wgt, pr
 
         early = [(j, c) for j in range(JT) for c in range(CHUNKS)][:8]
         for a in range(PASSES):
-            for j, c in early[:4]:
+            for j, c in early[:6]:
                 base(j, c, a)
 
         hc = sb.tile([P, S], U32, name="hc", align_bytes=64)
         hs = sb.tile([P, S], U8, name="hs", align_bytes=64)
         for j in range(JT):
             cols = slice(P * j, P * (j + 1))
-            bank = ps.tile([P, 4, P], F32, name=f"h{j}", tag=f"bank{4 + j % 4}")
+            bank = ps.tile([P, 4, P], F32, name=f"h{j}", tag=f"bank{6 + j % 2}")
             for t in range(4):
                 for a in range(PASSES):
                     nc.tensor.matmul_mx(
@@ -200,7 +201,7 @@ def tile_list_hlora_tm_res_kernel(tc, xT, w4_words, w4_scales, down, up, wgt, pr
                 out=hc[:, cols].bitcast(E4M3), scales=hs[:, cols], in_=hb[:].rearrange("p j t -> p (j t)")
             )
 
-        for j, c in early[4:]:
+        for j, c in early[6:]:
             base(j, c, 0)
             base(j, c, 1)
 

@@ -62,17 +62,17 @@ def tile_list_hlora_tm_res_kernel(tc, xT, w4_words, w4_scales, down, up, wgt, pr
         load_x(0, 3)
         load_x(1, 0)
         load_x(1, 1)
+        load_x(1, 2)
+        load_x(1, 3)
+        load_down(0)
         for r in range(4):
             nc.sync.dma_start(
                 out=w4s[r:P:32, :, :].bitcast(I32),
                 in_=w4_scales.bitcast(I32).rearrange("a (q r) n -> r q a n", r=4)[r],
             )
         load_w4(0)
-        load_x(1, 2)
-        load_x(1, 3)
-        load_down(0)
-        load_w4(1)
         load_down(1)
+        load_w4(1)
         uraw = {}
         cuts = (0, 512, 1024, 1536)
         for lo, hi in zip(cuts, cuts[1:]):
@@ -153,10 +153,12 @@ def tile_list_hlora_tm_res_kernel(tc, xT, w4_words, w4_scales, down, up, wgt, pr
         cast_x(scopy, 1, 0)
         cast_x(vcopy, 1, 1)
         quantize_x(1, 0)
-        cast_down(vcopy, 0, 0, P)
         quantize_x(1, 1)
-        cast_down(vcopy, 1, 0, P)
+        cast_down(scopy, 0, 0, 48)
+        cast_down(vcopy, 0, 48, P)
         quantize_down(0)
+        cast_down(scopy, 1, 0, 48)
+        cast_down(vcopy, 1, 48, P)
         quantize_down(1)
 
         acc = {}
@@ -185,15 +187,15 @@ def tile_list_hlora_tm_res_kernel(tc, xT, w4_words, w4_scales, down, up, wgt, pr
             cols = slice(P * j, P * (j + 1))
             bank = ps.tile([P, 4, P], F32, name=f"h{j}", tag=f"bank{6 + j % 2}")
             for t in range(4):
-                for a in range(PASSES):
+                for a in reversed(range(PASSES)):
                     nc.tensor.matmul_mx(
                         out=bank[:, t, :],
                         lhsT=dc[a][:, P * t : P * (t + 1)].bitcast(E4M3),
                         lhsT_scale=ds[a][:, P * t : P * (t + 1)],
                         rhs=xc[a][:, cols].bitcast(E4M3),
                         rhs_scale=xs[a][:, cols],
-                        start=(a == 0),
-                        stop=(a == PASSES - 1),
+                        start=(a == PASSES - 1),
+                        stop=(a == 0),
                     )
             hb = sb.tile([P, P, 4], BF16, name=f"hb{j}", align_bytes=64)
             scopy(out=hb[:], in_=bank[:].rearrange("p t j -> p j t"))
@@ -205,9 +207,11 @@ def tile_list_hlora_tm_res_kernel(tc, xT, w4_words, w4_scales, down, up, wgt, pr
             base(j, c, 0)
             base(j, c, 1)
 
-        for c, share in enumerate((256, 192, 256)):
-            cast_up(scopy, c, 0, share)
-            cast_up(vcopy, c, share, NC)
+        for c, share in enumerate((128, 128, 384)):
+            if share:
+                cast_up(scopy, c, 0, share)
+            if share < NC:
+                cast_up(vcopy, c, share, NC)
             quantize_up(c)
 
         def finish(j, c, res):
@@ -224,7 +228,7 @@ def tile_list_hlora_tm_res_kernel(tc, xT, w4_words, w4_scales, down, up, wgt, pr
                 stop=True,
             )
             residual = pv[j][:, NC * c : NC * (c + 1)]
-            if (j, c) in ((1, 0), (2, 0), (3, 0)):
+            if (j, c) in ((1, 1), (2, 1), (3, 0)):
                 y = sb.tile([P, NC], F32, name=f"y{j}{c}")
                 scopy(out=y[:], in_=acc[j, c][:])
                 nc.gpsimd.tensor_tensor(out=res, in0=y[:], in1=residual, op=mybir.AluOpType.add)

@@ -33,13 +33,14 @@ def tile_list_hlora_tm_res_kernel(tc, xT, w4_words, w4_scales, down, up, wgt, pr
     vcopy = nc.vector.tensor_copy
     with ExitStack() as ctx:
         sb = ctx.enter_context(tc.tile_pool(name="sb", bufs=1))
-        ps = ctx.enter_context(tc.psum_pool(name="ps", bufs=1))
+        ps = ctx.enter_context(tc.psum_pool(name="ps", bufs=8))
 
         lists = sb.tile([P, S // 16], U16, name="lists")
         w4s = sb.tile([P, PASSES, M], U8, name="w4s", align_bytes=64)
         nc.vector.memset(w4s[:].bitcast(I32), 0)
         wg = sb.tile([P, S], F32, name="wg")
-        planes, draw, w4, pv = {}, {}, {}, {}
+        w4 = sb.tile([P, PASSES, 2 * M], U8, name="w4", align_bytes=64)
+        planes, draw, pv = {}, {}, {}
 
         def load_x(a, i):
             planes[a, i] = sb.tile([P, T], F32, name=f"x{a}{i}")
@@ -49,10 +50,6 @@ def tile_list_hlora_tm_res_kernel(tc, xT, w4_words, w4_scales, down, up, wgt, pr
         def load_down(a):
             draw[a] = sb.tile([P, 4, R], F32, name=f"draw{a}")
             nc.sync.dma_start(out=draw[a][:], in_=down[512 * a : 512 * (a + 1), :].rearrange("(p j) r -> p j r", j=4))
-
-        def load_w4(a):
-            w4[a] = sb.tile([P, 2 * M], U8, name=f"w4{a}", align_bytes=64)
-            nc.sync.dma_start(out=w4[a][:].bitcast(I32), in_=w4_words.bitcast(I32)[a])
 
         nc.sync.dma_start(lists[:], offs)
         load_x(0, 0)
@@ -70,9 +67,8 @@ def tile_list_hlora_tm_res_kernel(tc, xT, w4_words, w4_scales, down, up, wgt, pr
                 out=w4s[r:P:32, :, :].bitcast(I32),
                 in_=w4_scales.bitcast(I32).rearrange("a (q r) n -> r q a n", r=4)[r],
             )
-        load_w4(0)
+        nc.sync.dma_start(out=w4[:].bitcast(I32), in_=w4_words.bitcast(I32).rearrange("a p n -> p a n"))
         load_down(1)
-        load_w4(1)
         uraw = {}
         cuts = (0, 512, 1024, 1536)
         for lo, hi in zip(cuts, cuts[1:]):
@@ -165,12 +161,12 @@ def tile_list_hlora_tm_res_kernel(tc, xT, w4_words, w4_scales, down, up, wgt, pr
 
         def base(j, c, a):
             if a == 0:
-                acc[j, c] = ps.tile([P, NC], F32, name=f"acc{j}{c}", tag=f"bank{(CHUNKS * j + c) % 8}")
+                acc[j, c] = ps.tile([P, NC], F32, name=f"acc{j}{c}", tag="bank")
             nc.tensor.matmul_mx(
                 out=acc[j, c][:],
                 lhsT=xc[a][:, P * j : P * (j + 1)].bitcast(E4M3),
                 lhsT_scale=xs[a][:, P * j : P * (j + 1)],
-                rhs=w4[a][:, 2 * NC * c : 2 * NC * (c + 1)].bitcast(E2M1),
+                rhs=w4[:, a, 2 * NC * c : 2 * NC * (c + 1)].bitcast(E2M1),
                 rhs_scale=w4s[:, a, NC * c : NC * (c + 1)],
                 start=(a == 0),
                 stop=False,
@@ -185,7 +181,7 @@ def tile_list_hlora_tm_res_kernel(tc, xT, w4_words, w4_scales, down, up, wgt, pr
         hs = sb.tile([P, S], U8, name="hs", align_bytes=64)
         for j in range(JT):
             cols = slice(P * j, P * (j + 1))
-            bank = ps.tile([P, 4, P], F32, name=f"h{j}", tag=f"bank{6 + j % 2}")
+            bank = ps.tile([P, 4, P], F32, name=f"h{j}", tag="bank")
             for t in range(4):
                 for a in reversed(range(PASSES)):
                     nc.tensor.matmul_mx(

@@ -1,6 +1,7 @@
 from contextlib import ExitStack
 
 import concourse.mybir as mybir
+from concourse.masks import make_identity
 
 K, R, M, T, S = 1024, 512, 1536, 1024, 512
 FLOPS = 2 * S * (K * R + K * M + R * M)
@@ -41,6 +42,10 @@ def tile_list_hlora_tm_res_kernel(tc, xT, w4_words, w4_scales, down, up, wgt, pr
         wg = sb.tile([P, S], F32, name="wg")
         w4 = sb.tile([P, PASSES, 2 * M], U8, name="w4", align_bytes=64)
         planes, draw, pv = {}, {}, {}
+        ident = sb.tile([P, P], F32, name="ident")
+        make_identity(nc, ident[:])
+        wrows = sb.tile([P, HALF], F32, name="wrows")
+        nc.gpsimd.memset(wrows[: P - 16, :], 0.0)
 
         def load_x(a, i):
             planes[a, i] = sb.tile([P, T], F32, name=f"x{a}{i}")
@@ -51,34 +56,61 @@ def tile_list_hlora_tm_res_kernel(tc, xT, w4_words, w4_scales, down, up, wgt, pr
             draw[a] = sb.tile([P, 4, R], F32, name=f"draw{a}")
             nc.sync.dma_start(out=draw[a][:], in_=down[512 * a : 512 * (a + 1), :].rearrange("(p j) r -> p j r", j=4))
 
+        uraw = {}
+
+        def load_scales():
+            for r in range(4):
+                nc.sync.dma_start(
+                    out=w4s[r:P:32, :, :].bitcast(I32),
+                    in_=w4_scales.bitcast(I32).rearrange("a (q r) n -> r q a n", r=4)[r],
+                )
+
+        def load_w4():
+            nc.sync.dma_start(out=w4[:].bitcast(I32), in_=w4_words.bitcast(I32).rearrange("a p n -> p a n"))
+
+        def load_up(first, last, lo, hi):
+            part = sb.tile([P, last - first, hi - lo], F32, name=f"uraw{first}{lo}")
+            nc.sync.dma_start(out=part[:], in_=up.rearrange("(p j) n -> p j n", j=4)[:, first:last, lo:hi])
+            for c in range(lo // NC, hi // NC):
+                uraw[first, c] = part[:, :, NC * c - lo : NC * (c + 1) - lo]
+
+        def load_prev(j):
+            pv[j] = sb.tile([P, M], F32, name=f"prev{j}")
+            nc.sync.dma_start(out=pv[j][:], in_=prev[P * j : P * (j + 1), :])
+
+        nc.sync.dma_start(out=wrows[P - 16 :, :], in_=wgt.rearrange("p (h j) -> (p h) j", h=2)[::17, :])
         nc.sync.dma_start(lists[:], offs)
         load_x(0, 0)
-        nc.sync.dma_start(out=wg[:], in_=wgt)
         load_x(0, 1)
         load_x(0, 2)
         load_x(0, 3)
         load_x(1, 0)
         load_x(1, 1)
+        load_down(0)
         load_x(1, 2)
         load_x(1, 3)
-        load_down(0)
-        for r in range(4):
-            nc.sync.dma_start(
-                out=w4s[r:P:32, :, :].bitcast(I32),
-                in_=w4_scales.bitcast(I32).rearrange("a (q r) n -> r q a n", r=4)[r],
-            )
-        nc.sync.dma_start(out=w4[:].bitcast(I32), in_=w4_words.bitcast(I32).rearrange("a p n -> p a n"))
+        load_scales()
+        load_w4()
         load_down(1)
-        uraw = {}
-        cuts = (0, 512, 1024, 1536)
-        for lo, hi in zip(cuts, cuts[1:]):
-            part = sb.tile([P, 4, hi - lo], F32, name=f"uraw{lo}")
-            nc.sync.dma_start(out=part[:], in_=up[:, lo:hi].rearrange("(p j) n -> p j n", j=4))
-            for c in range(lo // NC, hi // NC):
-                uraw[c] = part[:, :, NC * c - lo : NC * (c + 1) - lo]
+        load_up(0, 4, 0, 2 * NC)
+        load_up(0, 4, 2 * NC, M)
         for j in range(JT):
-            pv[j] = sb.tile([P, M], F32, name=f"prev{j}")
-            nc.sync.dma_start(out=pv[j][:], in_=prev[P * j : P * (j + 1), :])
+            load_prev(j)
+
+        turned = []
+        for c in range(2):
+            turned.append(ps.tile([P, P], F32, name=f"turned{c}", tag="bank"))
+            nc.tensor.transpose(turned[c][:], wrows[:, P * c : P * (c + 1)], ident[:])
+        for c, copy in enumerate((scopy, vcopy)):
+            wt = sb.tile([P, 2, 8, 16], F32, name=f"wt{c}")
+            copy(
+                out=wt[:],
+                in_=turned[c][:, P - 16 :].rearrange("p (g h) -> p h g", h=2).unsqueeze(3).to_broadcast([P, 2, 8, 16]),
+            )
+            back = ps.tile([P, 2, P], F32, name=f"back{c}", tag="bank")
+            for h in range(2):
+                nc.tensor.transpose(back[:, h, :], wt[:, h, :, :].rearrange("p g r -> p (g r)"), ident[:])
+            copy(out=wg[:].rearrange("p (h c j) -> p h c j", h=2, c=2)[:, :, c, :], in_=back[:])
 
         xc, xs, gath, xb = {}, {}, {}, {}
         for a in range(PASSES):
@@ -132,8 +164,8 @@ def tile_list_hlora_tm_res_kernel(tc, xT, w4_words, w4_scales, down, up, wgt, pr
             uc.append(sb.tile([P, NC], U32, name=f"uc{c}", align_bytes=64))
             us.append(sb.tile([P, NC], U8, name=f"us{c}", align_bytes=64))
 
-        def cast_up(copy, c, lo, hi):
-            interleave(copy, ub[c][:, lo:hi, :], uraw[c][:, :, lo:hi])
+        def cast_up(copy, first, last, c, lo, hi):
+            interleave(copy, ub[c][:, lo:hi, first:last], uraw[first, c][:, :, lo:hi])
 
         def quantize_up(c):
             nc.vector.quantize_mx(out=uc[c][:].bitcast(E4M3), scales=us[c][:], in_=ub[c][:].rearrange("p n j -> p (n j)"))
@@ -142,19 +174,18 @@ def tile_list_hlora_tm_res_kernel(tc, xT, w4_words, w4_scales, down, up, wgt, pr
             gather_plane(0, i)
         for h in range(2):
             cast_x(scopy, 0, h)
+        cast_down(scopy, 0, 0, P)
         for i in range(4):
             gather_plane(1, i)
             if i in (1, 2):
                 quantize_x(0, i - 1)
         cast_x(scopy, 1, 0)
         cast_x(vcopy, 1, 1)
+        quantize_down(0)
         quantize_x(1, 0)
         quantize_x(1, 1)
-        cast_down(scopy, 0, 0, 48)
-        cast_down(vcopy, 0, 48, P)
-        quantize_down(0)
-        cast_down(scopy, 1, 0, 48)
-        cast_down(vcopy, 1, 48, P)
+        cast_down(scopy, 1, 0, 40)
+        cast_down(vcopy, 1, 40, P)
         quantize_down(1)
 
         acc = {}
@@ -174,7 +205,7 @@ def tile_list_hlora_tm_res_kernel(tc, xT, w4_words, w4_scales, down, up, wgt, pr
 
         early = [(j, c) for j in range(JT) for c in range(CHUNKS)][:8]
         for a in range(PASSES):
-            for j, c in early[:6]:
+            for j, c in early[:4]:
                 base(j, c, a)
 
         hc = sb.tile([P, S], U32, name="hc", align_bytes=64)
@@ -199,16 +230,18 @@ def tile_list_hlora_tm_res_kernel(tc, xT, w4_words, w4_scales, down, up, wgt, pr
                 out=hc[:, cols].bitcast(E4M3), scales=hs[:, cols], in_=hb[:].rearrange("p j t -> p (j t)")
             )
 
-        for j, c in early[6:]:
+        for j, c in early[4:]:
             base(j, c, 0)
             base(j, c, 1)
 
-        for c, share in enumerate((128, 128, 384)):
-            if share:
-                cast_up(scopy, c, 0, share)
-            if share < NC:
-                cast_up(vcopy, c, share, NC)
-            quantize_up(c)
+        cast_up(vcopy, 0, 4, 0, 0, 512)
+        cast_up(scopy, 0, 4, 1, 0, 256)
+        cast_up(vcopy, 0, 4, 1, 256, 512)
+        quantize_up(0)
+        quantize_up(1)
+        cast_up(scopy, 0, 4, 2, 0, 384)
+        cast_up(vcopy, 0, 4, 2, 384, 512)
+        quantize_up(2)
 
         def finish(j, c, res):
             if (j, c) not in early:

@@ -235,12 +235,12 @@ def tile_list_hlora_tm_res_kernel(tc, xT, w4_words, w4_scales, down, up, wgt, pr
             base(j, c, 1)
 
         cast_up(vcopy, 0, 4, 0, 0, 512)
-        cast_up(scopy, 0, 4, 1, 0, 256)
-        cast_up(vcopy, 0, 4, 1, 256, 512)
+        cast_up(scopy, 0, 4, 1, 0, 192)
+        cast_up(vcopy, 0, 4, 1, 192, 512)
         quantize_up(0)
         quantize_up(1)
-        cast_up(scopy, 0, 4, 2, 0, 384)
-        cast_up(vcopy, 0, 4, 2, 384, 512)
+        cast_up(scopy, 0, 4, 2, 0, 256)
+        cast_up(vcopy, 0, 4, 2, 256, 512)
         quantize_up(2)
 
         def finish(j, c, res):

@@ -37,23 +37,23 @@ def tile_list_hlora_tm_res_kernel(tc, xT, w4_words, w4_scales, down, up, wgt, pr
         ps = ctx.enter_context(tc.psum_pool(name="ps", bufs=8))
 
         lists = sb.tile([P, S // 16], U16, name="lists")
-        w4s = sb.tile([P, PASSES, M], U8, name="w4s", align_bytes=64)
+        w4s = sb.tile([P, PASSES, M], U8, name="w4s", align_bytes=256)
         nc.vector.memset(w4s[:].bitcast(I32), 0)
-        wg = sb.tile([P, S], F32, name="wg")
-        w4 = sb.tile([P, PASSES, 2 * M], U8, name="w4", align_bytes=64)
+        wg = sb.tile([P, S], F32, name="wg", align_bytes=256)
+        w4 = sb.tile([P, PASSES, 2 * M], U8, name="w4", align_bytes=256)
         planes, draw, pv = {}, {}, {}
-        ident = sb.tile([P, P], F32, name="ident")
+        ident = sb.tile([P, P], F32, name="ident", align_bytes=256)
         make_identity(nc, ident[:])
-        wrows = sb.tile([P, HALF], F32, name="wrows")
+        wrows = sb.tile([P, HALF], F32, name="wrows", align_bytes=256)
         nc.gpsimd.memset(wrows[: P - 16, :], 0.0)
 
         def load_x(a, i):
-            planes[a, i] = sb.tile([P, T], F32, name=f"x{a}{i}")
+            planes[a, i] = sb.tile([P, T], F32, name=f"x{a}{i}", align_bytes=256)
             rows = xT[512 * a : 512 * (a + 1), :].rearrange("(p i) t -> p i t", i=4)
             nc.sync.dma_start(out=planes[a, i][:], in_=rows[:, i, :])
 
         def load_down(a):
-            draw[a] = sb.tile([P, 4, R], F32, name=f"draw{a}")
+            draw[a] = sb.tile([P, 4, R], F32, name=f"draw{a}", align_bytes=256)
             nc.sync.dma_start(out=draw[a][:], in_=down[512 * a : 512 * (a + 1), :].rearrange("(p j) r -> p j r", j=4))
 
         uraw = {}
@@ -69,18 +69,18 @@ def tile_list_hlora_tm_res_kernel(tc, xT, w4_words, w4_scales, down, up, wgt, pr
             nc.sync.dma_start(out=w4[:].bitcast(I32), in_=w4_words.bitcast(I32).rearrange("a p n -> p a n"))
 
         def load_up(first, last, lo, hi):
-            part = sb.tile([P, last - first, hi - lo], F32, name=f"uraw{first}{lo}")
+            part = sb.tile([P, last - first, hi - lo], F32, name=f"uraw{first}{lo}", align_bytes=256)
             nc.sync.dma_start(out=part[:], in_=up.rearrange("(p j) n -> p j n", j=4)[:, first:last, lo:hi])
             for c in range(lo // NC, hi // NC):
                 uraw[first, c] = part[:, :, NC * c - lo : NC * (c + 1) - lo]
 
         def load_prev(j):
-            pv[j] = sb.tile([P, M], F32, name=f"prev{j}")
+            pv[j] = sb.tile([P, M], F32, name=f"prev{j}", align_bytes=256)
             nc.sync.dma_start(out=pv[j][:], in_=prev[P * j : P * (j + 1), :])
 
         nc.sync.dma_start(out=wrows[P - 16 :, :], in_=wgt.rearrange("p (h j) -> (p h) j", h=2)[::17, :])
-        nc.sync.dma_start(lists[:], offs)
         load_x(0, 0)
+        nc.sync.dma_start(lists[:], offs)
         load_x(0, 1)
         load_x(0, 2)
         load_x(0, 3)
@@ -102,7 +102,7 @@ def tile_list_hlora_tm_res_kernel(tc, xT, w4_words, w4_scales, down, up, wgt, pr
             turned.append(ps.tile([P, P], F32, name=f"turned{c}", tag="bank"))
             nc.tensor.transpose(turned[c][:], wrows[:, P * c : P * (c + 1)], ident[:])
         for c, copy in enumerate((scopy, vcopy)):
-            wt = sb.tile([P, 2, 8, 16], F32, name=f"wt{c}")
+            wt = sb.tile([P, 2, 8, 16], F32, name=f"wt{c}", align_bytes=256)
             copy(
                 out=wt[:],
                 in_=turned[c][:, P - 16 :].rearrange("p (g h) -> p h g", h=2).unsqueeze(3).to_broadcast([P, 2, 8, 16]),
@@ -114,11 +114,11 @@ def tile_list_hlora_tm_res_kernel(tc, xT, w4_words, w4_scales, down, up, wgt, pr
 
         xc, xs, gath, xb = {}, {}, {}, {}
         for a in range(PASSES):
-            xc[a] = sb.tile([P, S], U32, name=f"xc{a}", align_bytes=64)
-            xs[a] = sb.tile([P, S], U8, name=f"xs{a}", align_bytes=64)
-            gath[a] = sb.tile([P, 4, S], F32, name=f"g{a}")
+            xc[a] = sb.tile([P, S], U32, name=f"xc{a}", align_bytes=256)
+            xs[a] = sb.tile([P, S], U8, name=f"xs{a}", align_bytes=256)
+            gath[a] = sb.tile([P, 4, S], F32, name=f"g{a}", align_bytes=256)
             for h in range(2):
-                xb[a, h] = sb.tile([P, HALF, 4], BF16, name=f"xb{a}{h}", align_bytes=64)
+                xb[a, h] = sb.tile([P, HALF, 4], BF16, name=f"xb{a}{h}", align_bytes=256)
 
         def gather(a, i, lo, hi):
             nc.vector.tensor_tensor(
@@ -143,9 +143,9 @@ def tile_list_hlora_tm_res_kernel(tc, xT, w4_words, w4_scales, down, up, wgt, pr
 
         dc, ds, db = {}, {}, {}
         for a in range(PASSES):
-            db[a] = sb.tile([P, R, 4], BF16, name=f"db{a}", align_bytes=64)
-            dc[a] = sb.tile([P, R], U32, name=f"dc{a}", align_bytes=64)
-            ds[a] = sb.tile([P, R], U8, name=f"ds{a}", align_bytes=64)
+            db[a] = sb.tile([P, R, 4], BF16, name=f"db{a}", align_bytes=256)
+            dc[a] = sb.tile([P, R], U32, name=f"dc{a}", align_bytes=256)
+            ds[a] = sb.tile([P, R], U8, name=f"ds{a}", align_bytes=256)
 
         def cast_down(copy, a, lo, hi):
             copy(
@@ -160,9 +160,9 @@ def tile_list_hlora_tm_res_kernel(tc, xT, w4_words, w4_scales, down, up, wgt, pr
 
         ub, uc, us = [], [], []
         for c in range(CHUNKS):
-            ub.append(sb.tile([P, NC, 4], BF16, name=f"ub{c}", align_bytes=64))
-            uc.append(sb.tile([P, NC], U32, name=f"uc{c}", align_bytes=64))
-            us.append(sb.tile([P, NC], U8, name=f"us{c}", align_bytes=64))
+            ub.append(sb.tile([P, NC, 4], BF16, name=f"ub{c}", align_bytes=256))
+            uc.append(sb.tile([P, NC], U32, name=f"uc{c}", align_bytes=256))
+            us.append(sb.tile([P, NC], U8, name=f"us{c}", align_bytes=256))
 
         def cast_up(copy, first, last, c, lo, hi):
             interleave(copy, ub[c][:, lo:hi, first:last], uraw[first, c][:, :, lo:hi])
@@ -208,8 +208,8 @@ def tile_list_hlora_tm_res_kernel(tc, xT, w4_words, w4_scales, down, up, wgt, pr
             for j, c in early[:4]:
                 base(j, c, a)
 
-        hc = sb.tile([P, S], U32, name="hc", align_bytes=64)
-        hs = sb.tile([P, S], U8, name="hs", align_bytes=64)
+        hc = sb.tile([P, S], U32, name="hc", align_bytes=256)
+        hs = sb.tile([P, S], U8, name="hs", align_bytes=256)
         for j in range(JT):
             cols = slice(P * j, P * (j + 1))
             bank = ps.tile([P, 4, P], F32, name=f"h{j}", tag="bank")
@@ -224,7 +224,7 @@ def tile_list_hlora_tm_res_kernel(tc, xT, w4_words, w4_scales, down, up, wgt, pr
                         start=(a == PASSES - 1),
                         stop=(a == 0),
                     )
-            hb = sb.tile([P, P, 4], BF16, name=f"hb{j}", align_bytes=64)
+            hb = sb.tile([P, P, 4], BF16, name=f"hb{j}", align_bytes=256)
             scopy(out=hb[:], in_=bank[:].rearrange("p t j -> p j t"))
             nc.vector.quantize_mx(
                 out=hc[:, cols].bitcast(E4M3), scales=hs[:, cols], in_=hb[:].rearrange("p j t -> p (j t)")
@@ -258,7 +258,7 @@ def tile_list_hlora_tm_res_kernel(tc, xT, w4_words, w4_scales, down, up, wgt, pr
             )
             residual = pv[j][:, NC * c : NC * (c + 1)]
             if (j, c) in ((1, 1), (2, 1), (3, 0)):
-                y = sb.tile([P, NC], F32, name=f"y{j}{c}")
+                y = sb.tile([P, NC], F32, name=f"y{j}{c}", align_bytes=256)
                 scopy(out=y[:], in_=acc[j, c][:])
                 nc.gpsimd.tensor_tensor(out=res, in0=y[:], in1=residual, op=mybir.AluOpType.add)
             else:
@@ -266,16 +266,16 @@ def tile_list_hlora_tm_res_kernel(tc, xT, w4_words, w4_scales, down, up, wgt, pr
 
         SPLIT = 2 * NC
         for j in range(2):
-            left = sb.tile([P, SPLIT], F32, name=f"left{j}")
+            left = sb.tile([P, SPLIT], F32, name=f"left{j}", align_bytes=256)
             for c in range(2):
                 finish(j, c, left[:, NC * c : NC * (c + 1)])
             nc.sync.dma_start(out=out[P * j : P * (j + 1), :SPLIT], in_=left[:])
-        right = sb.tile([P, 2, NC], F32, name="right")
+        right = sb.tile([P, 2, NC], F32, name="right", align_bytes=256)
         for j in range(2):
             finish(j, 2, right[:, j, :])
         nc.sync.dma_start(out=out[: 2 * P, SPLIT:].rearrange("(j p) n -> p j n", p=P), in_=right[:])
         for j in (2, 3):
-            res = sb.tile([P, M], F32, name=f"res{j}")
+            res = sb.tile([P, M], F32, name=f"res{j}", align_bytes=256)
             for c in range(CHUNKS):
                 finish(j, c, res[:, NC * c : NC * (c + 1)])
             nc.sync.dma_start(out=out[P * j : P * (j + 1), :], in_=res[:])

@@ -1,7 +1,6 @@
 from contextlib import ExitStack
 
 import concourse.mybir as mybir
-from concourse.masks import make_identity
 
 K, R, M, T, S = 1024, 512, 1536, 1024, 512
 FLOPS = 2 * S * (K * R + K * M + R * M)
@@ -42,10 +41,7 @@ def tile_list_hlora_tm_res_kernel(tc, xT, w4_words, w4_scales, down, up, wgt, pr
         wg = sb.tile([P, S], F32, name="wg", align_bytes=256)
         w4 = sb.tile([P, PASSES, 2 * M], U8, name="w4", align_bytes=256)
         planes, draw, pv = {}, {}, {}
-        ident = sb.tile([P, P], F32, name="ident", align_bytes=256)
-        make_identity(nc, ident[:])
-        wrows = sb.tile([P, HALF], F32, name="wrows", align_bytes=256)
-        nc.gpsimd.memset(wrows[: P - 16, :], 0.0)
+        wraw = sb.tile([P, 32], F32, name="wraw", align_bytes=256)
 
         def load_x(a, i):
             planes[a, i] = sb.tile([P, T], F32, name=f"x{a}{i}", align_bytes=256)
@@ -78,7 +74,8 @@ def tile_list_hlora_tm_res_kernel(tc, xT, w4_words, w4_scales, down, up, wgt, pr
             pv[j] = sb.tile([P, M], F32, name=f"prev{j}", align_bytes=256)
             nc.sync.dma_start(out=pv[j][:], in_=prev[P * j : P * (j + 1), :])
 
-        nc.sync.dma_start(out=wrows[P - 16 :, :], in_=wgt.rearrange("p (h j) -> (p h) j", h=2)[::17, :])
+        half_rows = wgt.rearrange("p (h j) -> (p h) j", h=2)[::17, :]
+        nc.sync.dma_start(out=wraw[:], in_=half_rows.rearrange("m (u c) -> m u c", c=32))
         load_x(0, 0)
         nc.sync.dma_start(lists[:], offs)
         load_x(0, 1)
@@ -86,31 +83,26 @@ def tile_list_hlora_tm_res_kernel(tc, xT, w4_words, w4_scales, down, up, wgt, pr
         load_x(0, 3)
         load_x(1, 0)
         load_x(1, 1)
-        load_down(0)
         load_x(1, 2)
+        load_down(0)
         load_x(1, 3)
+        load_down(1)
         load_scales()
         load_w4()
-        load_down(1)
         load_up(0, 4, 0, 2 * NC)
         load_up(0, 4, 2 * NC, M)
         for j in range(JT):
             load_prev(j)
 
-        turned = []
-        for c in range(2):
-            turned.append(ps.tile([P, P], F32, name=f"turned{c}", tag="bank"))
-            nc.tensor.transpose(turned[c][:], wrows[:, P * c : P * (c + 1)], ident[:])
-        for c, copy in enumerate((scopy, vcopy)):
-            wt = sb.tile([P, 2, 8, 16], F32, name=f"wt{c}", align_bytes=256)
-            copy(
-                out=wt[:],
-                in_=turned[c][:, P - 16 :].rearrange("p (g h) -> p h g", h=2).unsqueeze(3).to_broadcast([P, 2, 8, 16]),
-            )
-            back = ps.tile([P, 2, P], F32, name=f"back{c}", tag="bank")
-            for h in range(2):
-                nc.tensor.transpose(back[:, h, :], wt[:, h, :, :].rearrange("p g r -> p (g r)"), ident[:])
-            copy(out=wg[:].rearrange("p (h c j) -> p h c j", h=2, c=2)[:, :, c, :], in_=back[:])
+        turned = sb.tile([P, 32], F32, name="turned", align_bytes=256)
+        nc.vector.transpose(turned[:], wraw[:])
+        wide = []
+        for h in range(2):
+            wide.append(sb.tile([P, 8, 2, 16], F32, name=f"wide{h}", align_bytes=256))
+            picked = turned[:].rearrange("p (g r) -> p r g", g=2)[:, 8 * h : 8 * (h + 1), :]
+            vcopy(out=wide[h][:], in_=picked.unsqueeze(3).to_broadcast([P, 8, 2, 16]))
+        for h in range(2):
+            nc.vector.transpose(wg[:, HALF * h : HALF * (h + 1)], wide[h][:].rearrange("p r g e -> p (r g e)"))
 
         xc, xs, gath, xb = {}, {}, {}, {}
         for a in range(PASSES):
@@ -126,7 +118,7 @@ def tile_list_hlora_tm_res_kernel(tc, xT, w4_words, w4_scales, down, up, wgt, pr
             )
 
         def gather_plane(a, i):
-            if i < 3:
+            if (a, i) not in ((0, 0), (0, 3), (1, 3)):
                 gather(a, i, 0, S)
             else:
                 gather(a, i, 0, HALF)
@@ -179,13 +171,13 @@ def tile_list_hlora_tm_res_kernel(tc, xT, w4_words, w4_scales, down, up, wgt, pr
             gather_plane(1, i)
             if i in (1, 2):
                 quantize_x(0, i - 1)
-        cast_x(scopy, 1, 0)
-        cast_x(vcopy, 1, 1)
+        cast_x(vcopy, 1, 0)
+        cast_x(scopy, 1, 1)
         quantize_down(0)
         quantize_x(1, 0)
         quantize_x(1, 1)
-        cast_down(scopy, 1, 0, 40)
-        cast_down(vcopy, 1, 40, P)
+        cast_down(scopy, 1, 0, 56)
+        cast_down(vcopy, 1, 56, P)
         quantize_down(1)
 
         acc = {}
@@ -204,43 +196,46 @@ def tile_list_hlora_tm_res_kernel(tc, xT, w4_words, w4_scales, down, up, wgt, pr
             )
 
         early = [(j, c) for j in range(JT) for c in range(CHUNKS)][:8]
-        for a in range(PASSES):
-            for j, c in early[:4]:
-                base(j, c, a)
 
         hc = sb.tile([P, S], U32, name="hc", align_bytes=256)
         hs = sb.tile([P, S], U8, name="hs", align_bytes=256)
+        hbank = [ps.tile([P, 4, P], F32, name=f"h{j}", tag="bank") for j in range(JT)]
+
+        def h_pass(j, a):
+            cols = slice(P * j, P * (j + 1))
+            for t in range(4):
+                nc.tensor.matmul_mx(
+                    out=hbank[j][:, t, :],
+                    lhsT=dc[a][:, P * t : P * (t + 1)].bitcast(E4M3),
+                    lhsT_scale=ds[a][:, P * t : P * (t + 1)],
+                    rhs=xc[a][:, cols].bitcast(E4M3),
+                    rhs_scale=xs[a][:, cols],
+                    start=(a == 0 and t == 0),
+                    stop=(a == PASSES - 1 and t == 3),
+                )
+
+        for j in range(JT):
+            h_pass(j, 0)
         for j in range(JT):
             cols = slice(P * j, P * (j + 1))
-            bank = ps.tile([P, 4, P], F32, name=f"h{j}", tag="bank")
-            for t in range(4):
-                for a in reversed(range(PASSES)):
-                    nc.tensor.matmul_mx(
-                        out=bank[:, t, :],
-                        lhsT=dc[a][:, P * t : P * (t + 1)].bitcast(E4M3),
-                        lhsT_scale=ds[a][:, P * t : P * (t + 1)],
-                        rhs=xc[a][:, cols].bitcast(E4M3),
-                        rhs_scale=xs[a][:, cols],
-                        start=(a == PASSES - 1),
-                        stop=(a == 0),
-                    )
+            h_pass(j, 1)
             hb = sb.tile([P, P, 4], BF16, name=f"hb{j}", align_bytes=256)
-            scopy(out=hb[:], in_=bank[:].rearrange("p t j -> p j t"))
+            scopy(out=hb[:], in_=hbank[j][:].rearrange("p t j -> p j t"))
             nc.vector.quantize_mx(
                 out=hc[:, cols].bitcast(E4M3), scales=hs[:, cols], in_=hb[:].rearrange("p j t -> p (j t)")
             )
 
-        for j, c in early[4:]:
+        for j, c in early:
             base(j, c, 0)
             base(j, c, 1)
 
         cast_up(vcopy, 0, 4, 0, 0, 512)
-        cast_up(scopy, 0, 4, 1, 0, 192)
-        cast_up(vcopy, 0, 4, 1, 192, 512)
+        cast_up(scopy, 0, 4, 1, 0, 432)
+        cast_up(vcopy, 0, 4, 1, 432, 512)
         quantize_up(0)
         quantize_up(1)
-        cast_up(scopy, 0, 4, 2, 0, 256)
-        cast_up(vcopy, 0, 4, 2, 256, 512)
+        cast_up(scopy, 0, 4, 2, 0, 176)
+        cast_up(vcopy, 0, 4, 2, 176, 512)
         quantize_up(2)
 
         def finish(j, c, res):

@@ -39,7 +39,7 @@ def tile_list_hlora_tm_res_kernel(tc, xT, w4_words, w4_scales, down, up, wgt, pr
         w4s = sb.tile([P, PASSES, M], U8, name="w4s", align_bytes=256)
         nc.vector.memset(w4s[:].bitcast(I32), 0)
         wg = sb.tile([P, S], F32, name="wg", align_bytes=256)
-        w4 = sb.tile([P, PASSES, 2 * M], U8, name="w4", align_bytes=256)
+        w4 = {}
         planes, draw, pv = {}, {}, {}
         wraw = sb.tile([P, 32], F32, name="wraw", align_bytes=256)
 
@@ -61,8 +61,9 @@ def tile_list_hlora_tm_res_kernel(tc, xT, w4_words, w4_scales, down, up, wgt, pr
                     in_=w4_scales.bitcast(I32).rearrange("a (q r) n -> r q a n", r=4)[r],
                 )
 
-        def load_w4():
-            nc.sync.dma_start(out=w4[:].bitcast(I32), in_=w4_words.bitcast(I32).rearrange("a p n -> p a n"))
+        def load_w4(a):
+            w4[a] = sb.tile([P, 2 * M], U8, name=f"w4{a}", align_bytes=256)
+            nc.sync.dma_start(out=w4[a][:].bitcast(I32), in_=w4_words.bitcast(I32)[a])
 
         def load_up(first, last, lo, hi):
             part = sb.tile([P, last - first, hi - lo], F32, name=f"uraw{first}{lo}", align_bytes=256)
@@ -86,11 +87,11 @@ def tile_list_hlora_tm_res_kernel(tc, xT, w4_words, w4_scales, down, up, wgt, pr
         load_x(1, 2)
         load_down(0)
         load_x(1, 3)
-        load_down(1)
         load_scales()
-        load_w4()
-        load_up(0, 4, 0, 2 * NC)
-        load_up(0, 4, 2 * NC, M)
+        load_w4(0)
+        load_down(1)
+        load_up(0, 4, 0, M)
+        load_w4(1)
         for j in range(JT):
             load_prev(j)
 
@@ -189,7 +190,7 @@ def tile_list_hlora_tm_res_kernel(tc, xT, w4_words, w4_scales, down, up, wgt, pr
                 out=acc[j, c][:],
                 lhsT=xc[a][:, P * j : P * (j + 1)].bitcast(E4M3),
                 lhsT_scale=xs[a][:, P * j : P * (j + 1)],
-                rhs=w4[:, a, 2 * NC * c : 2 * NC * (c + 1)].bitcast(E2M1),
+                rhs=w4[a][:, 2 * NC * c : 2 * NC * (c + 1)].bitcast(E2M1),
                 rhs_scale=w4s[:, a, NC * c : NC * (c + 1)],
                 start=(a == 0),
                 stop=False,
@@ -216,6 +217,8 @@ def tile_list_hlora_tm_res_kernel(tc, xT, w4_words, w4_scales, down, up, wgt, pr
 
         for j in range(JT):
             h_pass(j, 0)
+        for j, c in early[:4]:
+            base(j, c, 0)
         for j in range(JT):
             cols = slice(P * j, P * (j + 1))
             h_pass(j, 1)
@@ -225,23 +228,22 @@ def tile_list_hlora_tm_res_kernel(tc, xT, w4_words, w4_scales, down, up, wgt, pr
                 out=hc[:, cols].bitcast(E4M3), scales=hs[:, cols], in_=hb[:].rearrange("p j t -> p (j t)")
             )
 
-        for j, c in early:
+        for j, c in early[4:]:
             base(j, c, 0)
-            base(j, c, 1)
 
         cast_up(vcopy, 0, 4, 0, 0, 512)
-        cast_up(scopy, 0, 4, 1, 0, 432)
-        cast_up(vcopy, 0, 4, 1, 432, 512)
+        cast_up(scopy, 0, 4, 1, 0, 448)
+        cast_up(vcopy, 0, 4, 1, 448, 512)
         quantize_up(0)
+        cast_up(scopy, 0, 4, 2, 0, 256)
+        cast_up(vcopy, 0, 4, 2, 256, 512)
         quantize_up(1)
-        cast_up(scopy, 0, 4, 2, 0, 176)
-        cast_up(vcopy, 0, 4, 2, 176, 512)
         quantize_up(2)
 
         def finish(j, c, res):
             if (j, c) not in early:
                 base(j, c, 0)
-                base(j, c, 1)
+            base(j, c, 1)
             nc.tensor.matmul_mx(
                 out=acc[j, c][:],
                 lhsT=hc[:, P * j : P * (j + 1)].bitcast(E4M3),
@@ -252,24 +254,14 @@ def tile_list_hlora_tm_res_kernel(tc, xT, w4_words, w4_scales, down, up, wgt, pr
                 stop=True,
             )
             residual = pv[j][:, NC * c : NC * (c + 1)]
-            if (j, c) in ((1, 1), (2, 1), (3, 0)):
+            if (j, c) in ((0, 0), (1, 0), (2, 0), (3, 0)):
                 y = sb.tile([P, NC], F32, name=f"y{j}{c}", align_bytes=256)
                 scopy(out=y[:], in_=acc[j, c][:])
                 nc.gpsimd.tensor_tensor(out=res, in0=y[:], in1=residual, op=mybir.AluOpType.add)
             else:
                 nc.vector.tensor_add(out=res, in0=acc[j, c][:], in1=residual)
 
-        SPLIT = 2 * NC
-        for j in range(2):
-            left = sb.tile([P, SPLIT], F32, name=f"left{j}", align_bytes=256)
-            for c in range(2):
-                finish(j, c, left[:, NC * c : NC * (c + 1)])
-            nc.sync.dma_start(out=out[P * j : P * (j + 1), :SPLIT], in_=left[:])
-        right = sb.tile([P, 2, NC], F32, name="right", align_bytes=256)
-        for j in range(2):
-            finish(j, 2, right[:, j, :])
-        nc.sync.dma_start(out=out[: 2 * P, SPLIT:].rearrange("(j p) n -> p j n", p=P), in_=right[:])
-        for j in (2, 3):
+        for j in range(JT):
             res = sb.tile([P, M], F32, name=f"res{j}", align_bytes=256)
             for c in range(CHUNKS):
                 finish(j, c, res[:, NC * c : NC * (c + 1)])

@@ -215,10 +215,10 @@ def tile_list_hlora_tm_res_kernel(tc, xT, w4_words, w4_scales, down, up, wgt, pr
                     stop=(a == PASSES - 1 and t == 3),
                 )
 
-        for j in range(JT):
-            h_pass(j, 0)
         for j, c in early[:4]:
             base(j, c, 0)
+        for j in range(JT):
+            h_pass(j, 0)
         for j in range(JT):
             cols = slice(P * j, P * (j + 1))
             h_pass(j, 1)
@@ -232,13 +232,11 @@ def tile_list_hlora_tm_res_kernel(tc, xT, w4_words, w4_scales, down, up, wgt, pr
             base(j, c, 0)
 
         cast_up(vcopy, 0, 4, 0, 0, 512)
-        cast_up(scopy, 0, 4, 1, 0, 448)
-        cast_up(vcopy, 0, 4, 1, 448, 512)
+        cast_up(scopy, 0, 4, 1, 0, 320)
+        cast_up(vcopy, 0, 4, 1, 320, 512)
         quantize_up(0)
-        cast_up(scopy, 0, 4, 2, 0, 256)
-        cast_up(vcopy, 0, 4, 2, 256, 512)
         quantize_up(1)
-        quantize_up(2)
+        cast_up(scopy, 0, 4, 2, 0, 512)
 
         def finish(j, c, res):
             if (j, c) not in early:
@@ -254,14 +252,22 @@ def tile_list_hlora_tm_res_kernel(tc, xT, w4_words, w4_scales, down, up, wgt, pr
                 stop=True,
             )
             residual = pv[j][:, NC * c : NC * (c + 1)]
-            if (j, c) in ((0, 0), (1, 0), (2, 0), (3, 0)):
+            if (j, c) in ((1, 1), (2, 0), (3, 0)):
                 y = sb.tile([P, NC], F32, name=f"y{j}{c}", align_bytes=256)
                 scopy(out=y[:], in_=acc[j, c][:])
                 nc.gpsimd.tensor_tensor(out=res, in0=y[:], in1=residual, op=mybir.AluOpType.add)
             else:
                 nc.vector.tensor_add(out=res, in0=acc[j, c][:], in1=residual)
 
-        for j in range(JT):
+        left = sb.tile([P, 2 * NC], F32, name="left", align_bytes=256)
+        for c in range(2):
+            finish(0, c, left[:, NC * c : NC * (c + 1)])
+        nc.sync.dma_start(out=out[:P, : 2 * NC], in_=left[:])
+        quantize_up(2)
+        right = sb.tile([P, NC], F32, name="right", align_bytes=256)
+        finish(0, 2, right[:])
+        nc.sync.dma_start(out=out[:P, 2 * NC :], in_=right[:])
+        for j in range(1, JT):
             res = sb.tile([P, M], F32, name=f"res{j}", align_bytes=256)
             for c in range(CHUNKS):
                 finish(j, c, res[:, NC * c : NC * (c + 1)])

@@ -36,8 +36,7 @@ def tile_list_hlora_tm_res_kernel(tc, xT, w4_words, w4_scales, down, up, wgt, pr
         ps = ctx.enter_context(tc.psum_pool(name="ps", bufs=8))
 
         lists = sb.tile([P, S // 16], U16, name="lists")
-        w4s = sb.tile([P, PASSES, M], U8, name="w4s", align_bytes=256)
-        nc.vector.memset(w4s[:].bitcast(I32), 0)
+        w4rows = sb.tile([P, PASSES, M], U8, name="w4rows", align_bytes=256)
         wg = sb.tile([P, S], F32, name="wg", align_bytes=256)
         w4 = {}
         planes, draw, pv = {}, {}, {}
@@ -57,7 +56,7 @@ def tile_list_hlora_tm_res_kernel(tc, xT, w4_words, w4_scales, down, up, wgt, pr
         def load_scales():
             for r in range(4):
                 nc.sync.dma_start(
-                    out=w4s[r:P:32, :, :].bitcast(I32),
+                    out=w4rows[r:P:32, :, :].bitcast(I32),
                     in_=w4_scales.bitcast(I32).rearrange("a (q r) n -> r q a n", r=4)[r],
                 )
 
@@ -77,8 +76,9 @@ def tile_list_hlora_tm_res_kernel(tc, xT, w4_words, w4_scales, down, up, wgt, pr
 
         half_rows = wgt.rearrange("p (h j) -> (p h) j", h=2)[::17, :]
         nc.sync.dma_start(out=wraw[:], in_=half_rows.rearrange("m (u c) -> m u c", c=32))
-        load_x(0, 0)
+        load_scales()
         nc.sync.dma_start(lists[:], offs)
+        load_x(0, 0)
         load_x(0, 1)
         load_x(0, 2)
         load_x(0, 3)
@@ -87,9 +87,8 @@ def tile_list_hlora_tm_res_kernel(tc, xT, w4_words, w4_scales, down, up, wgt, pr
         load_x(1, 2)
         load_down(0)
         load_x(1, 3)
-        load_scales()
-        load_w4(0)
         load_down(1)
+        load_w4(0)
         load_up(0, 4, 0, M)
         load_w4(1)
         for j in range(JT):
@@ -136,7 +135,7 @@ def tile_list_hlora_tm_res_kernel(tc, xT, w4_words, w4_scales, down, up, wgt, pr
 
         dc, ds, db = {}, {}, {}
         for a in range(PASSES):
-            db[a] = sb.tile([P, R, 4], BF16, name=f"db{a}", align_bytes=256)
+            db[a] = sb.tile([P, R, 4], BF16, name=f"db{a}", tag=f"db{a}", align_bytes=256)
             dc[a] = sb.tile([P, R], U32, name=f"dc{a}", align_bytes=256)
             ds[a] = sb.tile([P, R], U8, name=f"ds{a}", align_bytes=256)
 
@@ -181,6 +180,12 @@ def tile_list_hlora_tm_res_kernel(tc, xT, w4_words, w4_scales, down, up, wgt, pr
         cast_down(vcopy, 1, 56, P)
         quantize_down(1)
 
+        w4s = sb.tile([P, PASSES, M], U8, name="w4s", tag="db1", align_bytes=256)
+        nc.vector.memset(w4s[:].bitcast(I32), 0)
+        for q in range(4):
+            live = slice(32 * q, 32 * q + 4)
+            vcopy(out=w4s[live].bitcast(I32), in_=w4rows[live].bitcast(I32))
+
         acc = {}
 
         def base(j, c, a):
@@ -215,8 +220,6 @@ def tile_list_hlora_tm_res_kernel(tc, xT, w4_words, w4_scales, down, up, wgt, pr
                     stop=(a == PASSES - 1 and t == 3),
                 )
 
-        for j, c in early[:4]:
-            base(j, c, 0)
         for j in range(JT):
             h_pass(j, 0)
         for j in range(JT):
@@ -228,7 +231,7 @@ def tile_list_hlora_tm_res_kernel(tc, xT, w4_words, w4_scales, down, up, wgt, pr
                 out=hc[:, cols].bitcast(E4M3), scales=hs[:, cols], in_=hb[:].rearrange("p j t -> p (j t)")
             )
 
-        for j, c in early[4:]:
+        for j, c in early:
             base(j, c, 0)
 
         cast_up(vcopy, 0, 4, 0, 0, 512)

@@ -55,7 +55,7 @@ def tile_list_hlora_tm_res_kernel(tc, xT, w4_words, w4_scales, down, up, wgt, pr
 
         def load_scales():
             for r in range(4):
-                nc.sync.dma_start(
+                nc.gpsimd.dma_start(
                     out=w4rows[r:P:32, :, :].bitcast(I32),
                     in_=w4_scales.bitcast(I32).rearrange("a (q r) n -> r q a n", r=4)[r],
                 )
@@ -77,8 +77,8 @@ def tile_list_hlora_tm_res_kernel(tc, xT, w4_words, w4_scales, down, up, wgt, pr
         half_rows = wgt.rearrange("p (h j) -> (p h) j", h=2)[::17, :]
         nc.sync.dma_start(out=wraw[:], in_=half_rows.rearrange("m (u c) -> m u c", c=32))
         load_scales()
-        nc.sync.dma_start(lists[:], offs)
         load_x(0, 0)
+        nc.sync.dma_start(lists[:], offs)
         load_x(0, 1)
         load_x(0, 2)
         load_x(0, 3)

@@ -36,19 +36,23 @@ def tile_list_hlora_tm_res_kernel(tc, xT, w4_words, w4_scales, down, up, wgt, pr
         ps = ctx.enter_context(tc.psum_pool(name="ps", bufs=8))
 
         lists = sb.tile([P, S // 16], U16, name="lists")
-        w4rows = sb.tile([P, PASSES, M], U8, name="w4rows", align_bytes=256)
+        w4s = sb.tile([P, PASSES, M], U8, name="w4s", align_bytes=256)
         wg = sb.tile([P, S], F32, name="wg", align_bytes=256)
         w4 = {}
         planes, draw, pv = {}, {}, {}
         wraw = sb.tile([P, 32], F32, name="wraw", align_bytes=256)
 
         def load_x(a, i):
+            planes[a, i] = sb.tile([P, 2 * T], F32, name=f"x{a}{i}", tag=f"x{a}{i}", align_bytes=256)
+            rows = xT[512 * a : 512 * (a + 1), :].rearrange("(p u e) t -> p u (e t)", u=2, e=2)
+            nc.sync.dma_start(out=planes[a, i][:], in_=rows[:, i // 2, :])
+
+        def part_odd_plane(a, i):
             planes[a, i] = sb.tile([P, T], F32, name=f"x{a}{i}", align_bytes=256)
-            rows = xT[512 * a : 512 * (a + 1), :].rearrange("(p i) t -> p i t", i=4)
-            nc.sync.dma_start(out=planes[a, i][:], in_=rows[:, i, :])
+            scopy(out=planes[a, i][:], in_=planes[a, i - 1][:, T:])
 
         def load_down(a):
-            draw[a] = sb.tile([P, 4, R], F32, name=f"draw{a}", align_bytes=256)
+            draw[a] = sb.tile([P, 4, R], F32, name=f"draw{a}", tag=f"draw{a}", align_bytes=256)
             nc.sync.dma_start(out=draw[a][:], in_=down[512 * a : 512 * (a + 1), :].rearrange("(p j) r -> p j r", j=4))
 
         uraw = {}
@@ -56,43 +60,40 @@ def tile_list_hlora_tm_res_kernel(tc, xT, w4_words, w4_scales, down, up, wgt, pr
         def load_scales():
             for r in range(4):
                 nc.gpsimd.dma_start(
-                    out=w4rows[r:P:32, :, :].bitcast(I32),
+                    out=w4s[r:P:32, :, :].bitcast(I32),
                     in_=w4_scales.bitcast(I32).rearrange("a (q r) n -> r q a n", r=4)[r],
                 )
 
-        def load_w4(a):
-            w4[a] = sb.tile([P, 2 * M], U8, name=f"w4{a}", align_bytes=256)
+        def load_w4(a, tag):
+            w4[a] = sb.tile([P, 2 * M], U8, name=f"w4{a}", tag=tag, align_bytes=256)
             nc.sync.dma_start(out=w4[a][:].bitcast(I32), in_=w4_words.bitcast(I32)[a])
 
         def load_up(first, last, lo, hi):
-            part = sb.tile([P, last - first, hi - lo], F32, name=f"uraw{first}{lo}", align_bytes=256)
+            part = sb.tile([P, last - first, hi - lo], F32, name=f"uraw{first}{lo}", tag="x02", align_bytes=256)
             nc.sync.dma_start(out=part[:], in_=up.rearrange("(p j) n -> p j n", j=4)[:, first:last, lo:hi])
             for c in range(lo // NC, hi // NC):
                 uraw[first, c] = part[:, :, NC * c - lo : NC * (c + 1) - lo]
 
-        def load_prev(j):
-            pv[j] = sb.tile([P, M], F32, name=f"prev{j}", align_bytes=256)
-            nc.sync.dma_start(out=pv[j][:], in_=prev[P * j : P * (j + 1), :])
+        def token_rows(dram, h):
+            return dram[HALF * h : HALF * (h + 1), :].rearrange("(p e) n -> p e n", e=2)
+
+        def load_prev(h, tag):
+            pair = sb.tile([P, 2, M], F32, name=f"prev{h}", tag=tag, align_bytes=256)
+            nc.sync.dma_start(out=pair[:], in_=token_rows(prev, h))
+            for e in range(2):
+                pv[2 * h + e] = pair[:, e, :]
 
         half_rows = wgt.rearrange("p (h j) -> (p h) j", h=2)[::17, :]
         nc.sync.dma_start(out=wraw[:], in_=half_rows.rearrange("m (u c) -> m u c", c=32))
         load_scales()
         load_x(0, 0)
         nc.sync.dma_start(lists[:], offs)
-        load_x(0, 1)
         load_x(0, 2)
-        load_x(0, 3)
         load_x(1, 0)
-        load_x(1, 1)
         load_x(1, 2)
         load_down(0)
-        load_x(1, 3)
         load_down(1)
-        load_w4(0)
-        load_up(0, 4, 0, M)
-        load_w4(1)
-        for j in range(JT):
-            load_prev(j)
+        load_w4(0, "w40")
 
         turned = sb.tile([P, 32], F32, name="turned", align_bytes=256)
         nc.vector.transpose(turned[:], wraw[:])
@@ -109,8 +110,6 @@ def tile_list_hlora_tm_res_kernel(tc, xT, w4_words, w4_scales, down, up, wgt, pr
             xc[a] = sb.tile([P, S], U32, name=f"xc{a}", align_bytes=256)
             xs[a] = sb.tile([P, S], U8, name=f"xs{a}", align_bytes=256)
             gath[a] = sb.tile([P, 4, S], F32, name=f"g{a}", align_bytes=256)
-            for h in range(2):
-                xb[a, h] = sb.tile([P, HALF, 4], BF16, name=f"xb{a}{h}", align_bytes=256)
 
         def gather(a, i, lo, hi):
             nc.vector.tensor_tensor(
@@ -118,14 +117,20 @@ def tile_list_hlora_tm_res_kernel(tc, xT, w4_words, w4_scales, down, up, wgt, pr
             )
 
         def gather_plane(a, i):
+            if i % 2 == 0:
+                part_odd_plane(a, i + 1)
             if (a, i) not in ((0, 0), (0, 3), (1, 3)):
                 gather(a, i, 0, S)
             else:
                 gather(a, i, 0, HALF)
                 gather(a, i, HALF, S)
 
-        def cast_x(copy, a, h):
-            interleave(copy, xb[a, h][:], gath[a][:, :, h * HALF : (h + 1) * HALF])
+        def cast_x(copy, a, h, tag):
+            xb[a, h] = sb.tile([P, HALF, 4], BF16, name=f"xb{a}{h}", tag=tag, align_bytes=256)
+            copy(
+                out=xb[a, h][:].rearrange("p (e c i) t -> p c t i e", e=2, i=2),
+                in_=gath[a][:, :, h * HALF : (h + 1) * HALF].rearrange("p t (c i e) -> p c t i e", i=2, e=2),
+            )
 
         def quantize_x(a, h):
             cols = slice(h * HALF, (h + 1) * HALF)
@@ -164,27 +169,26 @@ def tile_list_hlora_tm_res_kernel(tc, xT, w4_words, w4_scales, down, up, wgt, pr
 
         for i in range(4):
             gather_plane(0, i)
-        for h in range(2):
-            cast_x(scopy, 0, h)
-        cast_down(scopy, 0, 0, P)
+        load_up(0, 4, 0, M)
         for i in range(4):
             gather_plane(1, i)
-            if i in (1, 2):
-                quantize_x(0, i - 1)
-        cast_x(vcopy, 1, 0)
-        cast_x(scopy, 1, 1)
+            if i in (0, 2):
+                cast_x(scopy, 0, i // 2, f"xb0{i // 2}")
+            if i in (1, 3):
+                quantize_x(0, i // 2)
+            if i == 1:
+                load_w4(1, "x10")
+        load_prev(0, "x12")
+        cast_down(scopy, 0, 0, P)
+        cast_x(vcopy, 1, 0, "xb10")
+        cast_x(scopy, 1, 1, "draw0")
         quantize_down(0)
         quantize_x(1, 0)
         quantize_x(1, 1)
+        load_prev(1, "draw0")
         cast_down(scopy, 1, 0, 56)
         cast_down(vcopy, 1, 56, P)
         quantize_down(1)
-
-        w4s = sb.tile([P, PASSES, M], U8, name="w4s", tag="db1", align_bytes=256)
-        nc.vector.memset(w4s[:].bitcast(I32), 0)
-        for q in range(4):
-            live = slice(32 * q, 32 * q + 4)
-            vcopy(out=w4s[live].bitcast(I32), in_=w4rows[live].bitcast(I32))
 
         acc = {}
 
@@ -220,6 +224,8 @@ def tile_list_hlora_tm_res_kernel(tc, xT, w4_words, w4_scales, down, up, wgt, pr
                     stop=(a == PASSES - 1 and t == 3),
                 )
 
+        for j, c in early[:4]:
+            base(j, c, 0)
         for j in range(JT):
             h_pass(j, 0)
         for j in range(JT):
@@ -231,15 +237,16 @@ def tile_list_hlora_tm_res_kernel(tc, xT, w4_words, w4_scales, down, up, wgt, pr
                 out=hc[:, cols].bitcast(E4M3), scales=hs[:, cols], in_=hb[:].rearrange("p j t -> p (j t)")
             )
 
-        for j, c in early:
+        for j, c in early[4:]:
             base(j, c, 0)
 
         cast_up(vcopy, 0, 4, 0, 0, 512)
-        cast_up(scopy, 0, 4, 1, 0, 320)
-        cast_up(vcopy, 0, 4, 1, 320, 512)
+        cast_up(scopy, 0, 4, 1, 0, 512)
         quantize_up(0)
+        cast_up(vcopy, 0, 4, 2, 160, 512)
+        cast_up(scopy, 0, 4, 2, 0, 160)
         quantize_up(1)
-        cast_up(scopy, 0, 4, 2, 0, 512)
+        quantize_up(2)
 
         def finish(j, c, res):
             if (j, c) not in early:
@@ -255,7 +262,7 @@ def tile_list_hlora_tm_res_kernel(tc, xT, w4_words, w4_scales, down, up, wgt, pr
                 stop=True,
             )
             residual = pv[j][:, NC * c : NC * (c + 1)]
-            if (j, c) in ((1, 1), (2, 0), (3, 0)):
+            if (j, c) in ((1, 0), (2, 0), (3, 0)):
                 y = sb.tile([P, NC], F32, name=f"y{j}{c}", align_bytes=256)
                 scopy(out=y[:], in_=acc[j, c][:])
                 nc.gpsimd.tensor_tensor(out=res, in0=y[:], in1=residual, op=mybir.AluOpType.add)
@@ -265,13 +272,12 @@ def tile_list_hlora_tm_res_kernel(tc, xT, w4_words, w4_scales, down, up, wgt, pr
         left = sb.tile([P, 2 * NC], F32, name="left", align_bytes=256)
         for c in range(2):
             finish(0, c, left[:, NC * c : NC * (c + 1)])
-        nc.sync.dma_start(out=out[:P, : 2 * NC], in_=left[:])
-        quantize_up(2)
+        nc.sync.dma_start(out=token_rows(out, 0)[:, 0, : 2 * NC], in_=left[:])
         right = sb.tile([P, NC], F32, name="right", align_bytes=256)
         finish(0, 2, right[:])
-        nc.sync.dma_start(out=out[:P, 2 * NC :], in_=right[:])
+        nc.sync.dma_start(out=token_rows(out, 0)[:, 0, 2 * NC :], in_=right[:])
         for j in range(1, JT):
             res = sb.tile([P, M], F32, name=f"res{j}", align_bytes=256)
             for c in range(CHUNKS):
                 finish(j, c, res[:, NC * c : NC * (c + 1)])
-            nc.sync.dma_start(out=out[P * j : P * (j + 1), :], in_=res[:])
+            nc.sync.dma_start(out=token_rows(out, j // 2)[:, j % 2, :], in_=res[:])

from contextlib import ExitStack

import concourse.mybir as mybir

K, R, M, T, S = 1024, 512, 1536, 1024, 512
FLOPS = 2 * S * (K * R + K * M + R * M)

F32 = mybir.dt.float32
BF16 = mybir.dt.bfloat16
I32 = mybir.dt.int32
U32 = mybir.dt.uint32
U16 = mybir.dt.uint16
U8 = mybir.dt.uint8
E4M3 = mybir.dt.float8_e4m3fn_x4
E2M1 = mybir.dt.float4_e2m1fn_x4
MULT = mybir.AluOpType.mult

P = 128
PASSES = K // 512
HALF = S // 2
NC = 512
CHUNKS = M // NC
JT = S // P


def interleave(copy, out, in_):
    copy(out=out.rearrange("p (c i) t -> p c t i", i=4), in_=in_.rearrange("p t (c i) -> p c t i", i=4))


def tile_list_hlora_tm_res_kernel(tc, xT, w4_words, w4_scales, down, up, wgt, prev, offs, out):
    nc = tc.nc
    scopy = nc.scalar.copy
    vcopy = nc.vector.tensor_copy
    with ExitStack() as ctx:
        sb = ctx.enter_context(tc.tile_pool(name="sb", bufs=1))
        ps = ctx.enter_context(tc.psum_pool(name="ps", bufs=8))

        lists = sb.tile([P, S // 16], U16, name="lists")
        w4s = sb.tile([P, PASSES, M], U8, name="w4s", align_bytes=256)
        wg = sb.tile([P, S], F32, name="wg", align_bytes=256)
        w4 = {}
        planes, draw, pv = {}, {}, {}
        wraw = sb.tile([P, 32], F32, name="wraw", align_bytes=256)

        def load_x(a, i):
            planes[a, i] = sb.tile([P, 2 * T], F32, name=f"x{a}{i}", tag=f"x{a}{i}", align_bytes=256)
            rows = xT[512 * a : 512 * (a + 1), :].rearrange("(p u e) t -> p u (e t)", u=2, e=2)
            nc.sync.dma_start(out=planes[a, i][:], in_=rows[:, i // 2, :])

        def part_odd_plane(a, i):
            planes[a, i] = sb.tile([P, T], F32, name=f"x{a}{i}", align_bytes=256)
            scopy(out=planes[a, i][:], in_=planes[a, i - 1][:, T:])

        def load_down(a):
            draw[a] = sb.tile([P, 4, R], F32, name=f"draw{a}", tag=f"draw{a}", align_bytes=256)
            nc.sync.dma_start(out=draw[a][:], in_=down[512 * a : 512 * (a + 1), :].rearrange("(p j) r -> p j r", j=4))

        uraw = {}

        def load_scales():
            for r in range(4):
                nc.gpsimd.dma_start(
                    out=w4s[r:P:32, :, :].bitcast(I32),
                    in_=w4_scales.bitcast(I32).rearrange("a (q r) n -> r q a n", r=4)[r],
                )

        def load_w4(a, tag):
            w4[a] = sb.tile([P, 2 * M], U8, name=f"w4{a}", tag=tag, align_bytes=256)
            nc.sync.dma_start(out=w4[a][:].bitcast(I32), in_=w4_words.bitcast(I32)[a])

        def load_up(first, last, lo, hi):
            part = sb.tile([P, last - first, hi - lo], F32, name=f"uraw{first}{lo}", tag="x02", align_bytes=256)
            nc.sync.dma_start(out=part[:], in_=up.rearrange("(p j) n -> p j n", j=4)[:, first:last, lo:hi])
            for c in range(lo // NC, hi // NC):
                uraw[first, c] = part[:, :, NC * c - lo : NC * (c + 1) - lo]

        def token_rows(dram, h):
            return dram[HALF * h : HALF * (h + 1), :].rearrange("(p e) n -> p e n", e=2)

        def load_prev(h, tag):
            pair = sb.tile([P, 2, M], F32, name=f"prev{h}", tag=tag, align_bytes=256)
            nc.sync.dma_start(out=pair[:], in_=token_rows(prev, h))
            for e in range(2):
                pv[2 * h + e] = pair[:, e, :]

        half_rows = wgt.rearrange("p (h j) -> (p h) j", h=2)[::17, :]
        nc.sync.dma_start(out=wraw[:], in_=half_rows.rearrange("m (u c) -> m u c", c=32))
        load_scales()
        load_x(0, 0)
        nc.sync.dma_start(lists[:], offs)
        load_x(0, 2)
        load_x(1, 0)
        load_x(1, 2)
        load_down(0)
        load_down(1)
        load_w4(0, "w40")

        turned = sb.tile([P, 32], F32, name="turned", align_bytes=256)
        nc.vector.transpose(turned[:], wraw[:])
        wide = []
        for h in range(2):
            wide.append(sb.tile([P, 8, 2, 16], F32, name=f"wide{h}", align_bytes=256))
            picked = turned[:].rearrange("p (g r) -> p r g", g=2)[:, 8 * h : 8 * (h + 1), :]
            vcopy(out=wide[h][:], in_=picked.unsqueeze(3).to_broadcast([P, 8, 2, 16]))
        for h in range(2):
            nc.vector.transpose(wg[:, HALF * h : HALF * (h + 1)], wide[h][:].rearrange("p r g e -> p (r g e)"))

        xc, xs, gath, xb = {}, {}, {}, {}
        for a in range(PASSES):
            xc[a] = sb.tile([P, S], U32, name=f"xc{a}", align_bytes=256)
            xs[a] = sb.tile([P, S], U8, name=f"xs{a}", align_bytes=256)
            gath[a] = sb.tile([P, 4, S], F32, name=f"g{a}", align_bytes=256)

        def gather(a, i, lo, hi):
            nc.vector.tensor_tensor(
                gath[a][:, i, lo:hi], planes[a, i][:].indirect(lists[:, lo // 16 : hi // 16]), wg[:, lo:hi], MULT
            )

        def gather_plane(a, i):
            if i % 2 == 0:
                part_odd_plane(a, i + 1)
            if (a, i) not in ((0, 0), (0, 3), (1, 3)):
                gather(a, i, 0, S)
            else:
                gather(a, i, 0, HALF)
                gather(a, i, HALF, S)

        def cast_x(copy, a, h, tag):
            xb[a, h] = sb.tile([P, HALF, 4], BF16, name=f"xb{a}{h}", tag=tag, align_bytes=256)
            copy(
                out=xb[a, h][:].rearrange("p (e c i) t -> p c t i e", e=2, i=2),
                in_=gath[a][:, :, h * HALF : (h + 1) * HALF].rearrange("p t (c i e) -> p c t i e", i=2, e=2),
            )

        def quantize_x(a, h):
            cols = slice(h * HALF, (h + 1) * HALF)
            nc.vector.quantize_mx(
                out=xc[a][:, cols].bitcast(E4M3), scales=xs[a][:, cols], in_=xb[a, h][:].rearrange("p j t -> p (j t)")
            )

        dc, ds, db = {}, {}, {}
        for a in range(PASSES):
            db[a] = sb.tile([P, R, 4], BF16, name=f"db{a}", tag=f"db{a}", align_bytes=256)
            dc[a] = sb.tile([P, R], U32, name=f"dc{a}", align_bytes=256)
            ds[a] = sb.tile([P, R], U8, name=f"ds{a}", align_bytes=256)

        def cast_down(copy, a, lo, hi):
            copy(
                out=db[a][:].rearrange("p (t m) j -> p m t j", t=4)[:, lo:hi],
                in_=draw[a][:].rearrange("p j (m t) -> p m t j", t=4)[:, lo:hi],
            )

        def quantize_down(a):
            nc.vector.quantize_mx(
                out=dc[a][:].bitcast(E4M3), scales=ds[a][:], in_=db[a][:].rearrange("p r j -> p (r j)")
            )

        ub, uc, us = [], [], []
        for c in range(CHUNKS):
            ub.append(sb.tile([P, NC, 4], BF16, name=f"ub{c}", align_bytes=256))
            uc.append(sb.tile([P, NC], U32, name=f"uc{c}", align_bytes=256))
            us.append(sb.tile([P, NC], U8, name=f"us{c}", align_bytes=256))

        def cast_up(copy, first, last, c, lo, hi):
            interleave(copy, ub[c][:, lo:hi, first:last], uraw[first, c][:, :, lo:hi])

        def quantize_up(c):
            nc.vector.quantize_mx(out=uc[c][:].bitcast(E4M3), scales=us[c][:], in_=ub[c][:].rearrange("p n j -> p (n j)"))

        for i in range(4):
            gather_plane(0, i)
        load_up(0, 4, 0, M)
        for i in range(4):
            gather_plane(1, i)
            if i in (0, 2):
                cast_x(scopy, 0, i // 2, f"xb0{i // 2}")
            if i in (1, 3):
                quantize_x(0, i // 2)
            if i == 1:
                load_w4(1, "x10")
        load_prev(0, "x12")
        cast_down(scopy, 0, 0, P)
        cast_x(vcopy, 1, 0, "xb10")
        cast_x(scopy, 1, 1, "draw0")
        quantize_down(0)
        quantize_x(1, 0)
        quantize_x(1, 1)
        load_prev(1, "draw0")
        cast_down(scopy, 1, 0, 56)
        cast_down(vcopy, 1, 56, P)
        quantize_down(1)

        acc = {}

        def base(j, c, a):
            if a == 0:
                acc[j, c] = ps.tile([P, NC], F32, name=f"acc{j}{c}", tag="bank")
            nc.tensor.matmul_mx(
                out=acc[j, c][:],
                lhsT=xc[a][:, P * j : P * (j + 1)].bitcast(E4M3),
                lhsT_scale=xs[a][:, P * j : P * (j + 1)],
                rhs=w4[a][:, 2 * NC * c : 2 * NC * (c + 1)].bitcast(E2M1),
                rhs_scale=w4s[:, a, NC * c : NC * (c + 1)],
                start=(a == 0),
                stop=False,
            )

        early = [(j, c) for j in range(JT) for c in range(CHUNKS)][:8]

        hc = sb.tile([P, S], U32, name="hc", align_bytes=256)
        hs = sb.tile([P, S], U8, name="hs", align_bytes=256)
        hbank = [ps.tile([P, 4, P], F32, name=f"h{j}", tag="bank") for j in range(JT)]

        def h_pass(j, a):
            cols = slice(P * j, P * (j + 1))
            for t in range(4):
                nc.tensor.matmul_mx(
                    out=hbank[j][:, t, :],
                    lhsT=dc[a][:, P * t : P * (t + 1)].bitcast(E4M3),
                    lhsT_scale=ds[a][:, P * t : P * (t + 1)],
                    rhs=xc[a][:, cols].bitcast(E4M3),
                    rhs_scale=xs[a][:, cols],
                    start=(a == 0 and t == 0),
                    stop=(a == PASSES - 1 and t == 3),
                )

        for j, c in early[:4]:
            base(j, c, 0)
        for j in range(JT):
            h_pass(j, 0)
        for j in range(JT):
            cols = slice(P * j, P * (j + 1))
            h_pass(j, 1)
            hb = sb.tile([P, P, 4], BF16, name=f"hb{j}", align_bytes=256)
            scopy(out=hb[:], in_=hbank[j][:].rearrange("p t j -> p j t"))
            nc.vector.quantize_mx(
                out=hc[:, cols].bitcast(E4M3), scales=hs[:, cols], in_=hb[:].rearrange("p j t -> p (j t)")
            )

        for j, c in early[4:]:
            base(j, c, 0)

        cast_up(vcopy, 0, 4, 0, 0, 512)
        cast_up(scopy, 0, 4, 1, 0, 512)
        quantize_up(0)
        cast_up(vcopy, 0, 4, 2, 160, 512)
        cast_up(scopy, 0, 4, 2, 0, 160)
        quantize_up(1)
        quantize_up(2)

        def finish(j, c, res):
            if (j, c) not in early:
                base(j, c, 0)
            base(j, c, 1)
            nc.tensor.matmul_mx(
                out=acc[j, c][:],
                lhsT=hc[:, P * j : P * (j + 1)].bitcast(E4M3),
                lhsT_scale=hs[:, P * j : P * (j + 1)],
                rhs=uc[c][:].bitcast(E4M3),
                rhs_scale=us[c][:],
                start=False,
                stop=True,
            )
            residual = pv[j][:, NC * c : NC * (c + 1)]
            if (j, c) in ((1, 0), (2, 0), (3, 0)):
                y = sb.tile([P, NC], F32, name=f"y{j}{c}", align_bytes=256)
                scopy(out=y[:], in_=acc[j, c][:])
                nc.gpsimd.tensor_tensor(out=res, in0=y[:], in1=residual, op=mybir.AluOpType.add)
            else:
                nc.vector.tensor_add(out=res, in0=acc[j, c][:], in1=residual)

        left = sb.tile([P, 2 * NC], F32, name="left", align_bytes=256)
        for c in range(2):
            finish(0, c, left[:, NC * c : NC * (c + 1)])
        nc.sync.dma_start(out=token_rows(out, 0)[:, 0, : 2 * NC], in_=left[:])
        right = sb.tile([P, NC], F32, name="right", align_bytes=256)
        finish(0, 2, right[:])
        nc.sync.dma_start(out=token_rows(out, 0)[:, 0, 2 * NC :], in_=right[:])
        for j in range(1, JT):
            res = sb.tile([P, M], F32, name=f"res{j}", align_bytes=256)
            for c in range(CHUNKS):
                finish(j, c, res[:, NC * c : NC * (c + 1)])
            nc.sync.dma_start(out=token_rows(out, j // 2)[:, j % 2, :], in_=res[:])
